import numpy as np
import ml_dtypes


def mxq(x, axis, fmt="e4m3"):
    dtype, down = {"e4m3": (ml_dtypes.float8_e4m3fn, 7), "e5m2": (ml_dtypes.float8_e5m2, 14)}[fmt]
    v = np.moveaxis(np.asarray(x, np.float32).astype(ml_dtypes.bfloat16).astype(np.float64), axis, -1)
    blocks = v.reshape(v.shape[:-1] + (-1, 32))
    amax = np.abs(blocks).max(-1, keepdims=True)
    byte = np.maximum(np.where(amax > 0, np.frexp(amax)[1] - 1 + 127, 0) - down, 1)
    scale = np.exp2(byte - 127.0)
    codes = (blocks / scale).astype(np.float32).astype(dtype).astype(np.float64)
    return np.moveaxis((codes * scale).reshape(v.shape), -1, axis)


WIDE = False


def mx_kscale(k):
    if not WIDE:
        return np.ones(k)
    levels = np.array([10, -10, 5, -5, 0])
    if k % 512:
        return np.exp2(np.random.permutation(np.resize(levels, k // 32))).repeat(32)
    a = np.empty((k // 512, 16))
    for p in range(k // 512):
        a[p, :8] = np.random.permutation(np.resize(levels, 8))
        for g in range(8):
            far = levels[np.abs(levels - a[p, g]) >= 10]
            a[p, g + 8] = far[np.random.randint(len(far))]
    return np.exp2(a.ravel()).repeat(32)


def f64(x):
    return np.asarray(x).astype(np.float64)


def striped(idx):
    return np.tile(idx.reshape(-1, 16).T, (8, 1)).astype(np.uint16)


def unstriped(offs):
    return offs[:16].T.reshape(-1).astype(np.int64)


E2M1 = np.array([0.0, 0.5, 1.0, 1.5, 2.0, 3.0, 4.0, 6.0, -0.0, -0.5, -1.0, -1.5, -2.0, -3.0, -4.0, -6.0])


def pack_weight(w, fmt):
    k, n = w.shape
    w = f64(np.asarray(w, np.float32).astype(ml_dtypes.bfloat16)).reshape(k // 32, 32, n)
    amax = np.abs(w).max(1)
    if fmt == "e4m3":
        byte = np.frexp(amax)[1] - 1 + 127 - 7
    else:
        mant, ex = np.frexp(amax / 6.0)
        byte = np.where(mant > 0.5, ex, ex - 1) + 127
    byte = np.clip(np.where(amax > 0, byte, 1), 1, 254)
    scaled = (w * np.exp2(127.0 - byte)[:, None, :]).reshape(k, n).astype(np.float32)
    by_word = np.ascontiguousarray(scaled.reshape(k // 512, 128, 4, n).transpose(0, 1, 3, 2))
    if fmt == "e4m3":
        words = by_word.astype(ml_dtypes.float8_e4m3fn).view(np.uint8)
    else:
        c = by_word.astype(ml_dtypes.float4_e2m1fn).view(np.uint8) & 0xF
        words = (c[..., 0::2] | (c[..., 1::2] << 4)).reshape(k // 512, 128, 2 * n)
    return np.ascontiguousarray(words), np.ascontiguousarray(byte.astype(np.uint8).reshape(k // 512, 16, n))


def unpack_weight(words, scales, fmt):
    g, _, n = scales.shape
    words = np.ascontiguousarray(words).reshape(g, 128, n, -1)
    if fmt == "e4m3":
        vals = words.view(ml_dtypes.float8_e4m3fn).astype(np.float64)
    else:
        nib = np.empty((g, 128, n, 4), np.uint8)
        nib[..., 0::2] = words & 0xF
        nib[..., 1::2] = words >> 4
        vals = E2M1[nib]
    vals = vals * np.repeat(np.exp2(scales.astype(np.float64) - 127.0), 8, axis=1)[..., None]
    return vals.transpose(0, 1, 3, 2).reshape(g * 512, n)


def gelu(v):
    return 0.5 * v * (1.0 + np.tanh(np.sqrt(2.0 / np.pi) * (v + 0.044715 * v**3)))


def striped8(idx):
    return np.concatenate([v.reshape(-1, 16).T for v in idx]).astype(np.uint16)


def unstriped8(offs):
    return np.stack([offs[16 * g:16 * g + 16].T.reshape(-1) for g in range(8)]).astype(np.int64)


def heads(xT, wgt, idx8):
    k = np.arange(xT.shape[0])
    return wgt[k // 4 % 128] * xT[k[:, None], idx8[k % 512 // 64]]


K, C, T, S, H, N = 1024, 512, 2048, 1024, 512, 384

def setup_inputs():
    n = np.random.standard_normal
    s, t, u = mx_kscale(K)[:, None], mx_kscale(C)[:, None], mx_kscale(H)[:, None]
    tab_words, tab_scales = pack_weight(n((C, T)) * t, "e4m3")
    w2_words, w2_scales = pack_weight(-n((C, H)) * 0.7 / np.sqrt(C) / t, "e2m1")
    w4_words, w4_scales = pack_weight(n((H, N)) * 1.5 / np.sqrt(H) / u, "e4m3")
    return {
        "xT": (n((K, T)) * s).astype(np.float32),
        "wgt": np.repeat(np.random.uniform(0.5, 2.0, (8, S)), 16, axis=0).astype(np.float32),
        "offs2": striped8(np.stack([np.random.permutation(T)[:S] for _ in range(8)])),
        "tab_words": tab_words, "tab_scales": tab_scales,
        "offs": striped(np.random.permutation(T)[:S]),
        "w1": (n((K, H)) * 0.7 / np.sqrt(K) / s).astype(np.float32),
        "w2_words": w2_words, "w2_scales": w2_scales,
        "w3": (n((K, N)) / np.sqrt(K) / s).astype(np.float32),
        "w4_words": w4_words, "w4_scales": w4_scales,
        "gain": (np.random.uniform(0.7, 1.5, H) * u[:, 0]).astype(np.float32),
    }

def reference(xT, wgt, offs2, tab_words, tab_scales, offs, w1, w2_words, w2_scales, w3, w4_words, w4_scales, gain):
    xg = mxq(heads(f64(xT), f64(wgt), unstriped8(offs2)), 0, "e4m3")
    v = unpack_weight(tab_words, tab_scales, "e4m3")[:, unstriped(offs)]
    w1q = mxq(f64(w1), 0, "e4m3")
    w2 = unpack_weight(w2_words, w2_scales, "e2m1")
    w3q = mxq(f64(w3), 0, "e4m3")
    w4 = unpack_weight(w4_words, w4_scales, "e4m3")
    d = w1q.T @ xg + w2.T @ v
    h = f64(gain)[:, None] * np.exp(-np.abs(d))
    hq = mxq(h, 0, "e4m3")
    y = w4.T @ hq
    r = w3q.T @ xg
    return y * r

@@ -1,0 +1,228 @@
+from contextlib import ExitStack
+
+import concourse.mybir as mybir
+
+K, C, T, S, H, N = 1024, 512, 2048, 1024, 512, 384
+FLOPS = 2 * S * (K * H + C * H + K * N + H * N)
+
+F32 = mybir.dt.float32
+BF16 = mybir.dt.bfloat16
+I32 = mybir.dt.int32
+U32 = mybir.dt.uint32
+U16 = mybir.dt.uint16
+U8 = mybir.dt.uint8
+FP8X4 = mybir.dt.float8_e4m3fn_x4
+FP4X4 = mybir.dt.float4_e2m1fn_x4
+MULT = mybir.AluOpType.mult
+ACT = mybir.ActivationFunctionType
+
+P = 128
+PACK = 4
+CHUNK = 256
+SUB = 128
+N_TILES = N // P
+
+
+def tile_list_template_contact_gate_kernel(
+    tc, xT, wgt, offs2, tab_words, tab_scales, offs, w1, w2_words, w2_scales, w3, w4_words, w4_scales, gain, out
+):
+    nc = tc.nc
+    with ExitStack() as ctx:
+        keep = ctx.enter_context(tc.tile_pool(name="keep", bufs=1))
+        ring = ctx.enter_context(tc.tile_pool(name="ring", bufs=2))
+        psum = ctx.enter_context(tc.psum_pool(name="psum", bufs=1))
+
+        def held(shape, dtype, name):
+            return keep.tile(shape, dtype, name=name, align_bytes=64)
+
+        def quantize(codes, scales, values):
+            nc.vector.quantize_mx(out=codes.bitcast(FP8X4), scales=scales, in_=values)
+
+        def load_scale_rows(queue, plane, rows):
+            for q in range(4):
+                queue.dma_start(out=plane[32 * q : 32 * q + 4, :].bitcast(I32), in_=rows[4 * q : 4 * q + 4, :].bitcast(I32))
+
+        def interleave(copy, dst, src):
+            copy(
+                out=dst.rearrange("p (c e i) -> p c i e", e=4, i=PACK),
+                in_=src.rearrange("p i (c e) -> p c i e", e=4),
+            )
+
+        def interleave_dealt(copy, dst, src):
+            copy(
+                out=dst.rearrange("p (t m i) -> p m i t", t=PACK, i=PACK),
+                in_=src.rearrange("p i (m t) -> p m i t", t=PACK),
+            )
+
+        offs_sb = held([P, S // 16], U16, "offs_sb")
+        offs2_sb = held([P, S // 16], U16, "offs2_sb")
+        tabw = held([P, T], U32, "tabw")
+        tabs = held([P, T], U8, "tabs")
+        wgt_sb = held([P, S], F32, "wgt_sb")
+        planes = [held([P, T], F32, f"plane{u}") for u in range(8)]
+        w1_raw = [held([P, PACK, H], F32, f"w1_raw{a}") for a in range(2)]
+        w3_raw = [held([P, PACK, N], F32, f"w3_raw{a}") for a in range(2)]
+        w2w_raw = held([P, 2 * H], U8, "w2w_raw")
+        w2s_raw = held([P, H], U8, "w2s_raw")
+        w4w = held([P, N], U32, "w4w")
+        w4s = held([P, N], U8, "w4s")
+        gain_sb = held([P, PACK], F32, "gain_sb")
+        warm_in = held([P, 1], F32, "warm_in")
+        warm_out = held([P, 1], F32, "warm_out")
+
+        nc.vector.memset(tabs[:].bitcast(I32), 0)
+        nc.vector.memset(warm_in[:], 0.0)
+        nc.vector.memset(w2s_raw[:].bitcast(I32), 0)
+        nc.vector.memset(w4s[:].bitcast(I32), 0)
+
+        x_rows = xT.rearrange("(a p i) t -> a i p t", a=2, i=PACK)
+        w1_rows = w1.rearrange("(a p i) r -> a p i r", a=2, i=PACK)
+        w3_rows = w3.rearrange("(a p i) n -> a p i n", a=2, i=PACK)
+
+        def load_plane(u):
+            nc.sync.dma_start(out=planes[u][:], in_=x_rows[u // PACK, u % PACK])
+
+        nc.sync.dma_start(offs_sb[:], offs)
+        load_scale_rows(nc.scalar, tabs, tab_scales[0])
+        nc.scalar.activation(out=warm_out[:], in_=warm_in[:], func=ACT.Exp)
+        nc.sync.dma_start(out=tabw[:].bitcast(I32), in_=tab_words[0].rearrange("p t i -> p (t i)").bitcast(I32))
+        nc.sync.dma_start(offs2_sb[:], offs2)
+        nc.sync.dma_start(out=wgt_sb[:], in_=wgt)
+        load_plane(0)
+        load_plane(1)
+        nc.sync.dma_start(out=w1_raw[0][:], in_=w1_rows[0])
+        load_plane(2)
+        load_plane(3)
+        nc.sync.dma_start(out=w2w_raw[:].bitcast(I32), in_=w2_words[0].bitcast(I32))
+        load_scale_rows(nc.sync, w2s_raw, w2_scales[0])
+        for u in range(4, 8):
+            load_plane(u)
+        nc.sync.dma_start(out=w1_raw[1][:], in_=w1_rows[1])
+        nc.sync.dma_start(out=gain_sb[:], in_=gain.rearrange("(p t) -> p t", t=PACK))
+        for a in range(2):
+            nc.sync.dma_start(out=w3_raw[a][:], in_=w3_rows[a])
+        nc.sync.dma_start(out=w4w[:].bitcast(I32), in_=w4_words[0].rearrange("p n i -> p (n i)").bitcast(I32))
+        load_scale_rows(nc.sync, w4s, w4_scales[0])
+
+        vs = held([P, S], U8, "vs")
+        vw = held([P, S], U32, "vw")
+        nc.vector.tensor_copy(vs[:], tabs[:].indirect(offs_sb[:]))
+        nc.vector.tensor_copy(vw[:], tabw[:].indirect(offs_sb[:]))
+
+        g0 = held([P, PACK, S], F32, "g0")
+        xq = [held([P, S], U32, f"xq{a}") for a in range(2)]
+        xs = [held([P, S], U8, f"xs{a}") for a in range(2)]
+        w1q = [held([P, H], U32, f"w1q{a}") for a in range(2)]
+        w1s = [held([P, H], U8, f"w1s{a}") for a in range(2)]
+        w3q = [held([P, N], U32, f"w3q{a}") for a in range(2)]
+        w3s = [held([P, N], U8, f"w3s{a}") for a in range(2)]
+        w1b = [held([P, PACK * H], BF16, f"w1b{a}") for a in range(2)]
+        w3b = [held([P, PACK * N], BF16, f"w3b{a}") for a in range(2)]
+        for i in range(PACK):
+            nc.vector.tensor_tensor(g0[:, i, :], planes[i][:].indirect(offs2_sb[:]), wgt_sb[:], MULT)
+        interleave_dealt(nc.scalar.copy, w1b[0][:], w1_raw[0][:])
+        quantize(w1q[0][:], w1s[0][:], w1b[0][:])
+        w2w = held([P, 2 * H], U8, "w2w")
+        w2s = held([P, H], U8, "w2s")
+        nc.vector.tensor_copy(
+            out=w2w[:].rearrange("p (t m b) -> p t m b", t=PACK, b=2),
+            in_=w2w_raw[:].rearrange("p (m t b) -> p t m b", t=PACK, b=2),
+        )
+        nc.vector.tensor_copy(
+            out=w2s[:].rearrange("p (t m) -> p t m", t=PACK), in_=w2s_raw[:].rearrange("p (m t) -> p t m", t=PACK)
+        )
+        xb0 = [held([P, PACK * 512], BF16, f"xb0_{h}") for h in range(2)]
+        for h in range(2):
+            interleave(nc.scalar.copy, xb0[h][:], g0[:, :, 512 * h : 512 * (h + 1)])
+
+        chunks = S // CHUNK
+        g1 = [held([P, PACK, CHUNK], F32, f"g1_{c}") for c in range(chunks)]
+
+        def gather1(i, c):
+            cols = slice(c * CHUNK, (c + 1) * CHUNK)
+            lists = offs2_sb[:, c * CHUNK // 16 : (c + 1) * CHUNK // 16]
+            nc.vector.tensor_tensor(g1[c][:, i, :], planes[PACK + i][:].indirect(lists), wgt_sb[:, cols], MULT)
+
+        for i in range(PACK - 1):
+            for c in range(chunks):
+                gather1(i, c)
+            if i < 2:
+                cols = slice(512 * i, 512 * (i + 1))
+                quantize(xq[0][:, cols], xs[0][:, cols], xb0[i][:])
+        xb1 = [held([P, PACK * CHUNK], BF16, f"xb1_{c}") for c in range(chunks)]
+        for c in range(chunks):
+            gather1(PACK - 1, c)
+            interleave(nc.scalar.copy, xb1[c][:], g1[c][:])
+        interleave_dealt(nc.vector.tensor_copy, w1b[1][:], w1_raw[1][:])
+        for c in range(chunks):
+            cols = slice(c * CHUNK, (c + 1) * CHUNK)
+            quantize(xq[1][:, cols], xs[1][:, cols], xb1[c][:])
+            if c == 0:
+                quantize(w1q[1][:], w1s[1][:], w1b[1][:])
+        for a in range(2):
+            interleave(nc.vector.tensor_copy, w3b[a][:], w3_raw[a][:])
+        for a in range(2):
+            quantize(w3q[a][:, :256], w3s[a][:, :256], w3b[a][:, :1024])
+            quantize(w3q[a][:, 256:], w3s[a][:, 256:], w3b[a][:, 1024:])
+
+        def mm(acc, lw, ls, rw, rs, start, stop):
+            nc.tensor.matmul_mx(out=acc, lhsT=lw, lhsT_scale=ls, rhs=rw, rhs_scale=rs, start=start, stop=stop)
+
+        out_rows = out.rearrange("(m p) j -> p m j", p=P)
+        gain_b = gain_sb[:].unsqueeze(1).to_broadcast([P, CHUNK, PACK])
+
+        def closeness(c):
+            absd = ring.tile([P, CHUNK * PACK], F32, name="absd")
+            for s in range(CHUNK // SUB):
+                cols = slice(c * CHUNK + s * SUB, c * CHUNK + (s + 1) * SUB)
+                d = psum.tile([P, PACK, SUB], F32, name="d", bufs=4)
+                for t in range(PACK):
+                    w = slice(t * P, (t + 1) * P)
+                    mm(d[:, t, :], w1q[0][:, w].bitcast(FP8X4), w1s[0][:, w], xq[0][:, cols].bitcast(FP8X4), xs[0][:, cols], t == 0, False)
+                for t in range(PACK):
+                    w = slice(t * P, (t + 1) * P)
+                    mm(d[:, t, :], w2w[:, 2 * t * P : 2 * (t + 1) * P].bitcast(FP4X4), w2s[:, w], vw[:, cols].bitcast(FP8X4), vs[:, cols], False, False)
+                for t in range(PACK):
+                    w = slice(t * P, (t + 1) * P)
+                    mm(d[:, t, :], w1q[1][:, w].bitcast(FP8X4), w1s[1][:, w], xq[1][:, cols].bitcast(FP8X4), xs[1][:, cols], False, t == PACK - 1)
+                nc.scalar.activation(
+                    out=absd[:, s * SUB * PACK : (s + 1) * SUB * PACK].rearrange("p (j t) -> p j t", t=PACK),
+                    in_=d[:].rearrange("p t j -> p j t"),
+                    func=ACT.Abs,
+                )
+            e = ring.tile([P, CHUNK * PACK], F32, name="e")
+            nc.scalar.activation(out=e[:], in_=absd[:], func=ACT.Exp, scale=-1.0)
+            hb = ring.tile([P, CHUNK * PACK], BF16, name="hb", align_bytes=64)
+            nc.vector.tensor_tensor(
+                hb[:].rearrange("p (j t) -> p j t", t=PACK), e[:].rearrange("p (j t) -> p j t", t=PACK), gain_b, MULT
+            )
+            hq = ring.tile([P, CHUNK], U32, name="hq", align_bytes=64)
+            hs = ring.tile([P, CHUNK], U8, name="hs", align_bytes=64)
+            quantize(hq[:], hs[:], hb[:])
+            return hq, hs
+
+        def finish(c, hq, hs):
+            ob = ring.tile([P, N_TILES, CHUNK], F32, name="ob")
+            for s in range(CHUNK // SUB):
+                cols = slice(c * CHUNK + s * SUB, c * CHUNK + (s + 1) * SUB)
+                sub = slice(s * SUB, (s + 1) * SUB)
+                r = psum.tile([P, N_TILES, SUB], F32, name="r", bufs=2)
+                for m in range(N_TILES):
+                    w = slice(m * P, (m + 1) * P)
+                    for a in range(2):
+                        mm(r[:, m, :], w3q[a][:, w].bitcast(FP8X4), w3s[a][:, w], xq[a][:, cols].bitcast(FP8X4), xs[a][:, cols], a == 0, a == 1)
+                r_sb = ring.tile([P, N_TILES, SUB], F32, name="r_sb", bufs=4)
+                nc.scalar.copy(out=r_sb[:], in_=r[:])
+                y = psum.tile([P, N_TILES, SUB], F32, name="y", bufs=2)
+                for m in range(N_TILES):
+                    w = slice(m * P, (m + 1) * P)
+                    mm(y[:, m, :], w4w[:, w].bitcast(FP8X4), w4s[:, w], hq[:, sub].bitcast(FP8X4), hs[:, sub], True, True)
+                nc.vector.tensor_tensor(ob[:, :, sub], y[:], r_sb[:], MULT)
+            nc.sync.dma_start(out=out_rows[:, :, c * CHUNK : (c + 1) * CHUNK], in_=ob[:])
+
+        made = {}
+        for c in range(chunks + 1):
+            if c < chunks:
+                made[c] = closeness(c)
+            if c >= 1:
+                finish(c - 1, *made[c - 1])

@@ -32,8 +32,8 @@ def tile_list_template_contact_gate_kernel(
         ring = ctx.enter_context(tc.tile_pool(name="ring", bufs=2))
         psum = ctx.enter_context(tc.psum_pool(name="psum", bufs=1))
 
-        def held(shape, dtype, name):
-            return keep.tile(shape, dtype, name=name, align_bytes=64)
+        def held(shape, dtype, name, tag=None):
+            return keep.tile(shape, dtype, name=name, tag=tag or name, align_bytes=64)
 
         def quantize(codes, scales, values):
             nc.vector.quantize_mx(out=codes.bitcast(FP8X4), scales=scales, in_=values)
@@ -70,7 +70,7 @@ def tile_list_template_contact_gate_kernel(
         warm_in = held([P, 1], F32, "warm_in")
         warm_out = held([P, 1], F32, "warm_out")
 
-        nc.vector.memset(tabs[:].bitcast(I32), 0)
+        nc.gpsimd.memset(tabs[:].bitcast(I32), 0)
         nc.vector.memset(warm_in[:], 0.0)
         nc.vector.memset(w2s_raw[:].bitcast(I32), 0)
         nc.vector.memset(w4s[:].bitcast(I32), 0)
@@ -82,38 +82,43 @@ def tile_list_template_contact_gate_kernel(
         def load_plane(u):
             nc.sync.dma_start(out=planes[u][:], in_=x_rows[u // PACK, u % PACK])
 
-        nc.sync.dma_start(offs_sb[:], offs)
-        load_scale_rows(nc.scalar, tabs, tab_scales[0])
         nc.scalar.activation(out=warm_out[:], in_=warm_in[:], func=ACT.Exp)
-        nc.sync.dma_start(out=tabw[:].bitcast(I32), in_=tab_words[0].rearrange("p t i -> p (t i)").bitcast(I32))
-        nc.sync.dma_start(offs2_sb[:], offs2)
+        nc.sync.dma_start(offs_sb[:], offs)
+        nc.sync.dma_start(out=w2w_raw[:].bitcast(I32), in_=w2_words[0].bitcast(I32))
         nc.sync.dma_start(out=wgt_sb[:], in_=wgt)
+        load_scale_rows(nc.sync, tabs, tab_scales[0])
         load_plane(0)
+        nc.sync.dma_start(offs2_sb[:], offs2)
         load_plane(1)
         nc.sync.dma_start(out=w1_raw[0][:], in_=w1_rows[0])
         load_plane(2)
         load_plane(3)
-        nc.sync.dma_start(out=w2w_raw[:].bitcast(I32), in_=w2_words[0].bitcast(I32))
         load_scale_rows(nc.sync, w2s_raw, w2_scales[0])
-        for u in range(4, 8):
-            load_plane(u)
+        load_plane(4)
         nc.sync.dma_start(out=w1_raw[1][:], in_=w1_rows[1])
+        load_plane(5)
+        load_plane(6)
+        nc.sync.dma_start(out=w3_raw[0][:], in_=w3_rows[0])
+        load_plane(7)
+        nc.sync.dma_start(out=tabw[:].bitcast(I32), in_=tab_words[0].rearrange("p t i -> p (t i)").bitcast(I32))
         nc.sync.dma_start(out=gain_sb[:], in_=gain.rearrange("(p t) -> p t", t=PACK))
-        for a in range(2):
-            nc.sync.dma_start(out=w3_raw[a][:], in_=w3_rows[a])
+        nc.sync.dma_start(out=w3_raw[1][:], in_=w3_rows[1])
         nc.sync.dma_start(out=w4w[:].bitcast(I32), in_=w4_words[0].rearrange("p n i -> p (n i)").bitcast(I32))
         load_scale_rows(nc.sync, w4s, w4_scales[0])
 
+        w2w = held([P, 2 * H], U8, "w2w")
+        w2s = held([P, H], U8, "w2s")
+        nc.vector.tensor_copy(
+            out=w2w[:].rearrange("p (t m b) -> p t m b", t=PACK, b=2),
+            in_=w2w_raw[:].rearrange("p (m t b) -> p t m b", t=PACK, b=2),
+        )
         vs = held([P, S], U8, "vs")
         vw = held([P, S], U32, "vw")
         nc.vector.tensor_copy(vs[:], tabs[:].indirect(offs_sb[:]))
-        nc.vector.tensor_copy(vw[:], tabw[:].indirect(offs_sb[:]))
 
         g0 = held([P, PACK, S], F32, "g0")
         xq = [held([P, S], U32, f"xq{a}") for a in range(2)]
-        xs = [held([P, S], U8, f"xs{a}") for a in range(2)]
         w1q = [held([P, H], U32, f"w1q{a}") for a in range(2)]
-        w1s = [held([P, H], U8, f"w1s{a}") for a in range(2)]
         w3q = [held([P, N], U32, f"w3q{a}") for a in range(2)]
         w3s = [held([P, N], U8, f"w3s{a}") for a in range(2)]
         w1b = [held([P, PACK * H], BF16, f"w1b{a}") for a in range(2)]
@@ -121,13 +126,8 @@ def tile_list_template_contact_gate_kernel(
         for i in range(PACK):
             nc.vector.tensor_tensor(g0[:, i, :], planes[i][:].indirect(offs2_sb[:]), wgt_sb[:], MULT)
         interleave_dealt(nc.scalar.copy, w1b[0][:], w1_raw[0][:])
+        w1s = [held([P, H], U8, "w1s0", "plane2")]
         quantize(w1q[0][:], w1s[0][:], w1b[0][:])
-        w2w = held([P, 2 * H], U8, "w2w")
-        w2s = held([P, H], U8, "w2s")
-        nc.vector.tensor_copy(
-            out=w2w[:].rearrange("p (t m b) -> p t m b", t=PACK, b=2),
-            in_=w2w_raw[:].rearrange("p (m t b) -> p t m b", t=PACK, b=2),
-        )
         nc.vector.tensor_copy(
             out=w2s[:].rearrange("p (t m) -> p t m", t=PACK), in_=w2s_raw[:].rearrange("p (m t) -> p t m", t=PACK)
         )
@@ -135,6 +135,8 @@ def tile_list_template_contact_gate_kernel(
         for h in range(2):
             interleave(nc.scalar.copy, xb0[h][:], g0[:, :, 512 * h : 512 * (h + 1)])
 
+        interleave_dealt(nc.scalar.copy, w1b[1][:], w1_raw[1][:])
+        interleave(nc.scalar.copy, w3b[0][:], w3_raw[0][:])
         chunks = S // CHUNK
         g1 = [held([P, PACK, CHUNK], F32, f"g1_{c}") for c in range(chunks)]
 
@@ -143,74 +145,83 @@ def tile_list_template_contact_gate_kernel(
             lists = offs2_sb[:, c * CHUNK // 16 : (c + 1) * CHUNK // 16]
             nc.vector.tensor_tensor(g1[c][:, i, :], planes[PACK + i][:].indirect(lists), wgt_sb[:, cols], MULT)
 
+        def quantize_w3(a):
+            quantize(w3q[a][:, :256], w3s[a][:, :256], w3b[a][:, :1024])
+            quantize(w3q[a][:, 256:], w3s[a][:, 256:], w3b[a][:, 1024:])
+
+        xs0 = []
         for i in range(PACK - 1):
             for c in range(chunks):
                 gather1(i, c)
             if i < 2:
-                cols = slice(512 * i, 512 * (i + 1))
-                quantize(xq[0][:, cols], xs[0][:, cols], xb0[i][:])
+                xs0.append(held([P, 512], U8, f"xs0_{i}", f"plane{PACK + i}"))
+                quantize(xq[0][:, 512 * i : 512 * (i + 1)], xs0[i][:], xb0[i][:])
+        w1s.append(held([P, H], U8, "w1s1", "plane6"))
+        quantize(w1q[1][:], w1s[1][:], w1b[1][:])
+        quantize_w3(0)
+        xs1 = held([P, S], U8, "xs1")
+
+        def xs(a, j, width):
+            return xs1[:, j : j + width] if a == 1 else xs0[j // 512][:, j % 512 : j % 512 + width]
+
         xb1 = [held([P, PACK * CHUNK], BF16, f"xb1_{c}") for c in range(chunks)]
         for c in range(chunks):
             gather1(PACK - 1, c)
             interleave(nc.scalar.copy, xb1[c][:], g1[c][:])
-        interleave_dealt(nc.vector.tensor_copy, w1b[1][:], w1_raw[1][:])
         for c in range(chunks):
             cols = slice(c * CHUNK, (c + 1) * CHUNK)
-            quantize(xq[1][:, cols], xs[1][:, cols], xb1[c][:])
-            if c == 0:
-                quantize(w1q[1][:], w1s[1][:], w1b[1][:])
-        for a in range(2):
-            interleave(nc.vector.tensor_copy, w3b[a][:], w3_raw[a][:])
-        for a in range(2):
-            quantize(w3q[a][:, :256], w3s[a][:, :256], w3b[a][:, :1024])
-            quantize(w3q[a][:, 256:], w3s[a][:, 256:], w3b[a][:, 1024:])
+            quantize(xq[1][:, cols], xs1[:, cols], xb1[c][:])
+            lists = offs_sb[:, c * CHUNK // 16 : (c + 1) * CHUNK // 16]
+            nc.vector.tensor_copy(vw[:, cols], tabw[:].indirect(lists))
+        interleave(nc.vector.tensor_copy, w3b[1][:], w3_raw[1][:])
+        quantize_w3(1)
 
         def mm(acc, lw, ls, rw, rs, start, stop):
             nc.tensor.matmul_mx(out=acc, lhsT=lw, lhsT_scale=ls, rhs=rw, rhs_scale=rs, start=start, stop=stop)
 
         out_rows = out.rearrange("(m p) j -> p m j", p=P)
-        gain_b = gain_sb[:].unsqueeze(1).to_broadcast([P, CHUNK, PACK])
 
-        def closeness(c):
-            absd = ring.tile([P, CHUNK * PACK], F32, name="absd")
-            for s in range(CHUNK // SUB):
-                cols = slice(c * CHUNK + s * SUB, c * CHUNK + (s + 1) * SUB)
+        def closeness(j0, width):
+            absd = ring.tile([P, width * PACK], F32, name="absd")
+            for s in range(width // SUB):
+                cols = slice(j0 + s * SUB, j0 + (s + 1) * SUB)
                 d = psum.tile([P, PACK, SUB], F32, name="d", bufs=4)
+                for a in range(2):
+                    for t in range(PACK):
+                        w = slice(t * P, (t + 1) * P)
+                        mm(d[:, t, :], w1q[a][:, w].bitcast(FP8X4), w1s[a][:, w], xq[a][:, cols].bitcast(FP8X4), xs(a, j0 + s * SUB, SUB), a == 0 and t == 0, False)
                 for t in range(PACK):
                     w = slice(t * P, (t + 1) * P)
-                    mm(d[:, t, :], w1q[0][:, w].bitcast(FP8X4), w1s[0][:, w], xq[0][:, cols].bitcast(FP8X4), xs[0][:, cols], t == 0, False)
-                for t in range(PACK):
-                    w = slice(t * P, (t + 1) * P)
-                    mm(d[:, t, :], w2w[:, 2 * t * P : 2 * (t + 1) * P].bitcast(FP4X4), w2s[:, w], vw[:, cols].bitcast(FP8X4), vs[:, cols], False, False)
-                for t in range(PACK):
-                    w = slice(t * P, (t + 1) * P)
-                    mm(d[:, t, :], w1q[1][:, w].bitcast(FP8X4), w1s[1][:, w], xq[1][:, cols].bitcast(FP8X4), xs[1][:, cols], False, t == PACK - 1)
+                    mm(d[:, t, :], w2w[:, 2 * t * P : 2 * (t + 1) * P].bitcast(FP4X4), w2s[:, w], vw[:, cols].bitcast(FP8X4), vs[:, cols], False, t == PACK - 1)
                 nc.scalar.activation(
                     out=absd[:, s * SUB * PACK : (s + 1) * SUB * PACK].rearrange("p (j t) -> p j t", t=PACK),
                     in_=d[:].rearrange("p t j -> p j t"),
                     func=ACT.Abs,
                 )
-            e = ring.tile([P, CHUNK * PACK], F32, name="e")
+            e = ring.tile([P, width * PACK], F32, name="e")
             nc.scalar.activation(out=e[:], in_=absd[:], func=ACT.Exp, scale=-1.0)
-            hb = ring.tile([P, CHUNK * PACK], BF16, name="hb", align_bytes=64)
+            hb = ring.tile([P, width * PACK], BF16, name="hb", align_bytes=64)
             nc.vector.tensor_tensor(
-                hb[:].rearrange("p (j t) -> p j t", t=PACK), e[:].rearrange("p (j t) -> p j t", t=PACK), gain_b, MULT
+                hb[:].rearrange("p (j t) -> p j t", t=PACK),
+                e[:].rearrange("p (j t) -> p j t", t=PACK),
+                gain_sb[:].unsqueeze(1).to_broadcast([P, width, PACK]),
+                MULT,
             )
-            hq = ring.tile([P, CHUNK], U32, name="hq", align_bytes=64)
-            hs = ring.tile([P, CHUNK], U8, name="hs", align_bytes=64)
+            hq = ring.tile([P, width], U32, name="hq", align_bytes=64)
+            hs = ring.tile([P, width], U8, name="hs", align_bytes=64)
             quantize(hq[:], hs[:], hb[:])
             return hq, hs
 
-        def finish(c, hq, hs):
-            ob = ring.tile([P, N_TILES, CHUNK], F32, name="ob")
-            for s in range(CHUNK // SUB):
-                cols = slice(c * CHUNK + s * SUB, c * CHUNK + (s + 1) * SUB)
+        def finish(j0, width, hq, hs):
+            ob = ring.tile([P, N_TILES, width], F32, name="ob", bufs=3)
+            for s in range(width // SUB):
+                cols = slice(j0 + s * SUB, j0 + (s + 1) * SUB)
                 sub = slice(s * SUB, (s + 1) * SUB)
                 r = psum.tile([P, N_TILES, SUB], F32, name="r", bufs=2)
                 for m in range(N_TILES):
                     w = slice(m * P, (m + 1) * P)
                     for a in range(2):
-                        mm(r[:, m, :], w3q[a][:, w].bitcast(FP8X4), w3s[a][:, w], xq[a][:, cols].bitcast(FP8X4), xs[a][:, cols], a == 0, a == 1)
+                        mm(r[:, m, :], w3q[a][:, w].bitcast(FP8X4), w3s[a][:, w], xq[a][:, cols].bitcast(FP8X4), xs(a, j0 + s * SUB, SUB), a == 0, a == 1)
                 r_sb = ring.tile([P, N_TILES, SUB], F32, name="r_sb", bufs=4)
                 nc.scalar.copy(out=r_sb[:], in_=r[:])
                 y = psum.tile([P, N_TILES, SUB], F32, name="y", bufs=2)
@@ -218,11 +229,12 @@ def tile_list_template_contact_gate_kernel(
                     w = slice(m * P, (m + 1) * P)
                     mm(y[:, m, :], w4w[:, w].bitcast(FP8X4), w4s[:, w], hq[:, sub].bitcast(FP8X4), hs[:, sub], True, True)
                 nc.vector.tensor_tensor(ob[:, :, sub], y[:], r_sb[:], MULT)
-            nc.sync.dma_start(out=out_rows[:, :, c * CHUNK : (c + 1) * CHUNK], in_=ob[:])
+            nc.sync.dma_start(out=out_rows[:, :, j0 : j0 + width], in_=ob[:])
 
-        made = {}
-        for c in range(chunks + 1):
-            if c < chunks:
-                made[c] = closeness(c)
-            if c >= 1:
-                finish(c - 1, *made[c - 1])
+        groups = [(0, 256), (256, 256), (512, 256), (768, 128), (896, 128)]
+        made = []
+        for g in range(len(groups) + 1):
+            if g < len(groups):
+                made.append(closeness(*groups[g]))
+            if g >= 1:
+                finish(*groups[g - 1], *made[g - 1])

@@ -72,8 +72,10 @@ def tile_list_template_contact_gate_kernel(
 
         nc.gpsimd.memset(tabs[:].bitcast(I32), 0)
         nc.vector.memset(warm_in[:], 0.0)
-        nc.vector.memset(w2s_raw[:].bitcast(I32), 0)
-        nc.vector.memset(w4s[:].bitcast(I32), 0)
+        nc.gpsimd.memset(w2s_raw[:].bitcast(I32), 0)
+        nc.gpsimd.memset(w4s[:].bitcast(I32), 0)
+        load_scale_rows(nc.gpsimd, w4s, w4_scales[0])
+        nc.gpsimd.dma_start(out=gain_sb[:], in_=gain.rearrange("(p t) -> p t", t=PACK))
 
         x_rows = xT.rearrange("(a p i) t -> a i p t", a=2, i=PACK)
         w1_rows = w1.rearrange("(a p i) r -> a p i r", a=2, i=PACK)
@@ -85,26 +87,24 @@ def tile_list_template_contact_gate_kernel(
         nc.scalar.activation(out=warm_out[:], in_=warm_in[:], func=ACT.Exp)
         nc.sync.dma_start(offs_sb[:], offs)
         nc.sync.dma_start(out=w2w_raw[:].bitcast(I32), in_=w2_words[0].bitcast(I32))
-        nc.sync.dma_start(out=wgt_sb[:], in_=wgt)
+        nc.sync.dma_start(out=wgt_sb[:, :512], in_=wgt[:, :512])
         load_scale_rows(nc.sync, tabs, tab_scales[0])
         load_plane(0)
         nc.sync.dma_start(offs2_sb[:], offs2)
-        load_plane(1)
-        nc.sync.dma_start(out=w1_raw[0][:], in_=w1_rows[0])
-        load_plane(2)
-        load_plane(3)
+        nc.sync.dma_start(out=wgt_sb[:, 512:], in_=wgt[:, 512:])
+        for u in range(1, 4):
+            load_plane(u)
         load_scale_rows(nc.sync, w2s_raw, w2_scales[0])
         load_plane(4)
-        nc.sync.dma_start(out=w1_raw[1][:], in_=w1_rows[1])
+        nc.sync.dma_start(out=w1_raw[0][:], in_=w1_rows[0])
         load_plane(5)
+        nc.sync.dma_start(out=w1_raw[1][:], in_=w1_rows[1])
         load_plane(6)
-        nc.sync.dma_start(out=w3_raw[0][:], in_=w3_rows[0])
         load_plane(7)
         nc.sync.dma_start(out=tabw[:].bitcast(I32), in_=tab_words[0].rearrange("p t i -> p (t i)").bitcast(I32))
-        nc.sync.dma_start(out=gain_sb[:], in_=gain.rearrange("(p t) -> p t", t=PACK))
-        nc.sync.dma_start(out=w3_raw[1][:], in_=w3_rows[1])
+        for a in range(2):
+            nc.sync.dma_start(out=w3_raw[a][:], in_=w3_rows[a])
         nc.sync.dma_start(out=w4w[:].bitcast(I32), in_=w4_words[0].rearrange("p n i -> p (n i)").bitcast(I32))
-        load_scale_rows(nc.sync, w4s, w4_scales[0])
 
         w2w = held([P, 2 * H], U8, "w2w")
         w2s = held([P, H], U8, "w2s")
@@ -123,11 +123,11 @@ def tile_list_template_contact_gate_kernel(
         w3s = [held([P, N], U8, f"w3s{a}") for a in range(2)]
         w1b = [held([P, PACK * H], BF16, f"w1b{a}") for a in range(2)]
         w3b = [held([P, PACK * N], BF16, f"w3b{a}") for a in range(2)]
-        for i in range(PACK):
+        for h in range(2):
+            cols = slice(512 * h, 512 * (h + 1))
+            nc.vector.tensor_tensor(g0[:, 0, cols], planes[0][:].indirect(offs2_sb[:, 32 * h : 32 * (h + 1)]), wgt_sb[:, cols], MULT)
+        for i in range(1, PACK):
             nc.vector.tensor_tensor(g0[:, i, :], planes[i][:].indirect(offs2_sb[:]), wgt_sb[:], MULT)
-        interleave_dealt(nc.scalar.copy, w1b[0][:], w1_raw[0][:])
-        w1s = [held([P, H], U8, "w1s0", "plane2")]
-        quantize(w1q[0][:], w1s[0][:], w1b[0][:])
         nc.vector.tensor_copy(
             out=w2s[:].rearrange("p (t m) -> p t m", t=PACK), in_=w2s_raw[:].rearrange("p (m t) -> p t m", t=PACK)
         )
@@ -135,30 +135,33 @@ def tile_list_template_contact_gate_kernel(
         for h in range(2):
             interleave(nc.scalar.copy, xb0[h][:], g0[:, :, 512 * h : 512 * (h + 1)])
 
-        interleave_dealt(nc.scalar.copy, w1b[1][:], w1_raw[1][:])
-        interleave(nc.scalar.copy, w3b[0][:], w3_raw[0][:])
+        for a in range(2):
+            interleave_dealt(nc.scalar.copy, w1b[a][:], w1_raw[a][:])
         chunks = S // CHUNK
-        g1 = [held([P, PACK, CHUNK], F32, f"g1_{c}") for c in range(chunks)]
+        g1 = [held([P, PACK, 512], F32, f"g1_{h}") for h in range(2)]
 
-        def gather1(i, c):
-            cols = slice(c * CHUNK, (c + 1) * CHUNK)
-            lists = offs2_sb[:, c * CHUNK // 16 : (c + 1) * CHUNK // 16]
-            nc.vector.tensor_tensor(g1[c][:, i, :], planes[PACK + i][:].indirect(lists), wgt_sb[:, cols], MULT)
+        def gather1(i, j, width):
+            lists = offs2_sb[:, j // 16 : (j + width) // 16]
+            picked = g1[j // 512][:, i, j % 512 : j % 512 + width]
+            nc.vector.tensor_tensor(picked, planes[PACK + i][:].indirect(lists), wgt_sb[:, j : j + width], MULT)
 
         def quantize_w3(a):
             quantize(w3q[a][:, :256], w3s[a][:, :256], w3b[a][:, :1024])
             quantize(w3q[a][:, 256:], w3s[a][:, 256:], w3b[a][:, 1024:])
 
-        xs0 = []
-        for i in range(PACK - 1):
-            for c in range(chunks):
-                gather1(i, c)
-            if i < 2:
-                xs0.append(held([P, 512], U8, f"xs0_{i}", f"plane{PACK + i}"))
-                quantize(xq[0][:, 512 * i : 512 * (i + 1)], xs0[i][:], xb0[i][:])
-        w1s.append(held([P, H], U8, "w1s1", "plane6"))
-        quantize(w1q[1][:], w1s[1][:], w1b[1][:])
-        quantize_w3(0)
+        for h in range(2):
+            gather1(0, 512 * h, 512)
+        xs0 = [held([P, 512], U8, "xs0_0", "plane4")]
+        quantize(xq[0][:, :512], xs0[0][:], xb0[0][:])
+        for h in range(2):
+            gather1(1, 512 * h, 512)
+        after5 = held([P, 1024], U8, "after5", "plane5")
+        xs0.append(after5[:, :512])
+        w1s = [after5[:, 512:]]
+        quantize(xq[0][:, 512:], xs0[1], xb0[1][:])
+        quantize(w1q[0][:], w1s[0], w1b[0][:])
+        for h in range(2):
+            gather1(2, 512 * h, 512)
         xs1 = held([P, S], U8, "xs1")
 
         def xs(a, j, width):
@@ -166,15 +169,20 @@ def tile_list_template_contact_gate_kernel(
 
         xb1 = [held([P, PACK * CHUNK], BF16, f"xb1_{c}") for c in range(chunks)]
         for c in range(chunks):
-            gather1(PACK - 1, c)
-            interleave(nc.scalar.copy, xb1[c][:], g1[c][:])
+            j = c * CHUNK
+            gather1(PACK - 1, j, CHUNK)
+            interleave(nc.scalar.copy, xb1[c][:], g1[j // 512][:, :, j % 512 : j % 512 + CHUNK])
+        w1s.append(held([P, H], U8, "w1s1", "plane7"))
+        quantize(w1q[1][:], w1s[1][:], w1b[1][:])
         for c in range(chunks):
             cols = slice(c * CHUNK, (c + 1) * CHUNK)
             quantize(xq[1][:, cols], xs1[:, cols], xb1[c][:])
             lists = offs_sb[:, c * CHUNK // 16 : (c + 1) * CHUNK // 16]
             nc.vector.tensor_copy(vw[:, cols], tabw[:].indirect(lists))
+        interleave(nc.scalar.copy, w3b[0][:], w3_raw[0][:])
         interleave(nc.vector.tensor_copy, w3b[1][:], w3_raw[1][:])
-        quantize_w3(1)
+        for a in range(2):
+            quantize_w3(a)
 
         def mm(acc, lw, ls, rw, rs, start, stop):
             nc.tensor.matmul_mx(out=acc, lhsT=lw, lhsT_scale=ls, rhs=rw, rhs_scale=rs, start=start, stop=stop)

@@ -155,32 +155,31 @@ def tile_list_template_contact_gate_kernel(
         quantize(xq[0][:, :512], xs0[0][:], xb0[0][:])
         for h in range(2):
             gather1(1, 512 * h, 512)
-        after5 = held([P, 1024], U8, "after5", "plane5")
-        xs0.append(after5[:, :512])
-        w1s = [after5[:, 512:]]
-        quantize(xq[0][:, 512:], xs0[1], xb0[1][:])
-        quantize(w1q[0][:], w1s[0], w1b[0][:])
+        xs0.append(held([P, 512], U8, "xs0_1", "plane5"))
+        quantize(xq[0][:, 512:], xs0[1][:], xb0[1][:])
         for h in range(2):
             gather1(2, 512 * h, 512)
+        w1s_both = held([P, 2 * H], U8, "w1s_both", "plane6")
+        w1s = [w1s_both[:, a * H : (a + 1) * H] for a in range(2)]
+        for a in range(2):
+            quantize(w1q[a][:], w1s[a], w1b[a][:])
         xs1 = held([P, S], U8, "xs1")
 
         def xs(a, j, width):
             return xs1[:, j : j + width] if a == 1 else xs0[j // 512][:, j % 512 : j % 512 + width]
 
-        xb1 = [held([P, PACK * CHUNK], BF16, f"xb1_{c}") for c in range(chunks)]
+        for c in range(chunks):
+            gather1(PACK - 1, c * CHUNK, CHUNK)
         for c in range(chunks):
             j = c * CHUNK
-            gather1(PACK - 1, j, CHUNK)
-            interleave(nc.scalar.copy, xb1[c][:], g1[j // 512][:, :, j % 512 : j % 512 + CHUNK])
-        w1s.append(held([P, H], U8, "w1s1", "plane7"))
-        quantize(w1q[1][:], w1s[1][:], w1b[1][:])
-        for c in range(chunks):
-            cols = slice(c * CHUNK, (c + 1) * CHUNK)
-            quantize(xq[1][:, cols], xs1[:, cols], xb1[c][:])
-            lists = offs_sb[:, c * CHUNK // 16 : (c + 1) * CHUNK // 16]
-            nc.vector.tensor_copy(vw[:, cols], tabw[:].indirect(lists))
-        interleave(nc.scalar.copy, w3b[0][:], w3_raw[0][:])
-        interleave(nc.vector.tensor_copy, w3b[1][:], w3_raw[1][:])
+            cols = slice(j, j + CHUNK)
+            xb1 = ring.tile([P, PACK * CHUNK], BF16, name="xb1", align_bytes=64)
+            copy = nc.vector.tensor_copy if c == chunks - 1 else nc.scalar.copy
+            interleave(copy, xb1[:], g1[j // 512][:, :, j % 512 : j % 512 + CHUNK])
+            quantize(xq[1][:, cols], xs1[:, cols], xb1[:])
+            nc.vector.tensor_copy(vw[:, cols], tabw[:].indirect(offs_sb[:, j // 16 : (j + CHUNK) // 16]))
+        for a in range(2):
+            interleave(nc.vector.tensor_copy, w3b[a][:], w3_raw[a][:])
         for a in range(2):
             quantize_w3(a)
 

@@ -67,11 +67,8 @@ def tile_list_template_contact_gate_kernel(
         w4w = held([P, N], U32, "w4w")
         w4s = held([P, N], U8, "w4s")
         gain_sb = held([P, PACK], F32, "gain_sb")
-        warm_in = held([P, 1], F32, "warm_in")
-        warm_out = held([P, 1], F32, "warm_out")
 
         nc.gpsimd.memset(tabs[:].bitcast(I32), 0)
-        nc.vector.memset(warm_in[:], 0.0)
         nc.gpsimd.memset(w2s_raw[:].bitcast(I32), 0)
         nc.gpsimd.memset(w4s[:].bitcast(I32), 0)
         load_scale_rows(nc.gpsimd, w4s, w4_scales[0])
@@ -84,9 +81,7 @@ def tile_list_template_contact_gate_kernel(
         def load_plane(u):
             nc.sync.dma_start(out=planes[u][:], in_=x_rows[u // PACK, u % PACK])
 
-        nc.scalar.activation(out=warm_out[:], in_=warm_in[:], func=ACT.Exp)
         nc.sync.dma_start(offs_sb[:], offs)
-        nc.sync.dma_start(out=w2w_raw[:].bitcast(I32), in_=w2_words[0].bitcast(I32))
         nc.sync.dma_start(out=wgt_sb[:, :512], in_=wgt[:, :512])
         load_scale_rows(nc.sync, tabs, tab_scales[0])
         load_plane(0)
@@ -94,24 +89,19 @@ def tile_list_template_contact_gate_kernel(
         nc.sync.dma_start(out=wgt_sb[:, 512:], in_=wgt[:, 512:])
         for u in range(1, 4):
             load_plane(u)
+        nc.sync.dma_start(out=w2w_raw[:].bitcast(I32), in_=w2_words[0].bitcast(I32))
         load_scale_rows(nc.sync, w2s_raw, w2_scales[0])
         load_plane(4)
-        nc.sync.dma_start(out=w1_raw[0][:], in_=w1_rows[0])
         load_plane(5)
-        nc.sync.dma_start(out=w1_raw[1][:], in_=w1_rows[1])
+        nc.sync.dma_start(out=w1_raw[0][:], in_=w1_rows[0])
         load_plane(6)
         load_plane(7)
+        nc.sync.dma_start(out=w1_raw[1][:], in_=w1_rows[1])
         nc.sync.dma_start(out=tabw[:].bitcast(I32), in_=tab_words[0].rearrange("p t i -> p (t i)").bitcast(I32))
         for a in range(2):
             nc.sync.dma_start(out=w3_raw[a][:], in_=w3_rows[a])
         nc.sync.dma_start(out=w4w[:].bitcast(I32), in_=w4_words[0].rearrange("p n i -> p (n i)").bitcast(I32))
 
-        w2w = held([P, 2 * H], U8, "w2w")
-        w2s = held([P, H], U8, "w2s")
-        nc.vector.tensor_copy(
-            out=w2w[:].rearrange("p (t m b) -> p t m b", t=PACK, b=2),
-            in_=w2w_raw[:].rearrange("p (m t b) -> p t m b", t=PACK, b=2),
-        )
         vs = held([P, S], U8, "vs")
         vw = held([P, S], U32, "vw")
         nc.vector.tensor_copy(vs[:], tabs[:].indirect(offs_sb[:]))
@@ -128,58 +118,57 @@ def tile_list_template_contact_gate_kernel(
             nc.vector.tensor_tensor(g0[:, 0, cols], planes[0][:].indirect(offs2_sb[:, 32 * h : 32 * (h + 1)]), wgt_sb[:, cols], MULT)
         for i in range(1, PACK):
             nc.vector.tensor_tensor(g0[:, i, :], planes[i][:].indirect(offs2_sb[:]), wgt_sb[:], MULT)
-        nc.vector.tensor_copy(
-            out=w2s[:].rearrange("p (t m) -> p t m", t=PACK), in_=w2s_raw[:].rearrange("p (m t) -> p t m", t=PACK)
-        )
         xb0 = [held([P, PACK * 512], BF16, f"xb0_{h}") for h in range(2)]
         for h in range(2):
             interleave(nc.scalar.copy, xb0[h][:], g0[:, :, 512 * h : 512 * (h + 1)])
-
-        for a in range(2):
-            interleave_dealt(nc.scalar.copy, w1b[a][:], w1_raw[a][:])
+        interleave_dealt(nc.scalar.copy, w1b[0][:], w1_raw[0][:])
         chunks = S // CHUNK
-        g1 = [held([P, PACK, 512], F32, f"g1_{h}") for h in range(2)]
+        g1 = held([P, PACK, S], F32, "g1")
 
         def gather1(i, j, width):
             lists = offs2_sb[:, j // 16 : (j + width) // 16]
-            picked = g1[j // 512][:, i, j % 512 : j % 512 + width]
-            nc.vector.tensor_tensor(picked, planes[PACK + i][:].indirect(lists), wgt_sb[:, j : j + width], MULT)
+            nc.vector.tensor_tensor(g1[:, i, j : j + width], planes[PACK + i][:].indirect(lists), wgt_sb[:, j : j + width], MULT)
 
         def quantize_w3(a):
             quantize(w3q[a][:, :256], w3s[a][:, :256], w3b[a][:, :1024])
             quantize(w3q[a][:, 256:], w3s[a][:, 256:], w3b[a][:, 1024:])
 
+        gather1(0, 0, S)
+        w2_both = held([P, 3 * H], U8, "w2_both", "plane4")
+        w2w = w2_both[:, : 2 * H]
+        w2s = w2_both[:, 2 * H :]
+        gather1(1, 0, S)
+        nc.vector.tensor_copy(
+            out=w2w.rearrange("p (t m b) -> p t m b", t=PACK, b=2),
+            in_=w2w_raw[:].rearrange("p (m t b) -> p t m b", t=PACK, b=2),
+        )
+        nc.vector.tensor_copy(out=w2s.rearrange("p (t m) -> p t m", t=PACK), in_=w2s_raw[:].rearrange("p (m t) -> p t m", t=PACK))
+        xs0 = held([P, S], U8, "xs0", "plane5")
         for h in range(2):
-            gather1(0, 512 * h, 512)
-        xs0 = [held([P, 512], U8, "xs0_0", "plane4")]
-        quantize(xq[0][:, :512], xs0[0][:], xb0[0][:])
-        for h in range(2):
-            gather1(1, 512 * h, 512)
-        xs0.append(held([P, 512], U8, "xs0_1", "plane5"))
-        quantize(xq[0][:, 512:], xs0[1][:], xb0[1][:])
-        for h in range(2):
-            gather1(2, 512 * h, 512)
-        w1s_both = held([P, 2 * H], U8, "w1s_both", "plane6")
+            quantize(xq[0][:, 512 * h : 512 * (h + 1)], xs0[:, 512 * h : 512 * (h + 1)], xb0[h][:])
+        gather1(2, 0, S)
+        for c in range(chunks):
+            gather1(PACK - 1, c * CHUNK, CHUNK)
+        w1s_both = held([P, 2 * H], U8, "w1s_both", "plane7")
         w1s = [w1s_both[:, a * H : (a + 1) * H] for a in range(2)]
-        for a in range(2):
-            quantize(w1q[a][:], w1s[a], w1b[a][:])
+        quantize(w1q[0][:], w1s[0], w1b[0][:])
+        interleave_dealt(nc.vector.tensor_copy, w1b[1][:], w1_raw[1][:])
         xs1 = held([P, S], U8, "xs1")
 
         def xs(a, j, width):
-            return xs1[:, j : j + width] if a == 1 else xs0[j // 512][:, j % 512 : j % 512 + width]
+            return (xs0, xs1)[a][:, j : j + width]
 
-        for c in range(chunks):
-            gather1(PACK - 1, c * CHUNK, CHUNK)
         for c in range(chunks):
             j = c * CHUNK
             cols = slice(j, j + CHUNK)
-            xb1 = ring.tile([P, PACK * CHUNK], BF16, name="xb1", align_bytes=64)
-            copy = nc.vector.tensor_copy if c == chunks - 1 else nc.scalar.copy
-            interleave(copy, xb1[:], g1[j // 512][:, :, j % 512 : j % 512 + CHUNK])
+            xb1 = ring.tile([P, PACK * CHUNK], BF16, name="xb1", align_bytes=64, bufs=4)
+            interleave(nc.scalar.copy, xb1[:], g1[:, :, cols])
             quantize(xq[1][:, cols], xs1[:, cols], xb1[:])
+            if c == 0:
+                quantize(w1q[1][:], w1s[1], w1b[1][:])
             nc.vector.tensor_copy(vw[:, cols], tabw[:].indirect(offs_sb[:, j // 16 : (j + CHUNK) // 16]))
-        for a in range(2):
-            interleave(nc.vector.tensor_copy, w3b[a][:], w3_raw[a][:])
+        interleave(nc.vector.tensor_copy, w3b[0][:], w3_raw[0][:])
+        interleave(nc.vector.tensor_copy, w3b[1][:], w3_raw[1][:])
         for a in range(2):
             quantize_w3(a)
 

@@ -38,9 +38,8 @@ def tile_list_template_contact_gate_kernel(
         def quantize(codes, scales, values):
             nc.vector.quantize_mx(out=codes.bitcast(FP8X4), scales=scales, in_=values)
 
-        def load_scale_rows(queue, plane, rows):
-            for q in range(4):
-                queue.dma_start(out=plane[32 * q : 32 * q + 4, :].bitcast(I32), in_=rows[4 * q : 4 * q + 4, :].bitcast(I32))
+        def load_scale_quadrant(plane, rows, q):
+            nc.sync.dma_start(out=plane[32 * q : 32 * q + 4, :].bitcast(I32), in_=rows[4 * q : 4 * q + 4, :].bitcast(I32))
 
         def interleave(copy, dst, src):
             copy(
@@ -71,8 +70,6 @@ def tile_list_template_contact_gate_kernel(
         nc.gpsimd.memset(tabs[:].bitcast(I32), 0)
         nc.gpsimd.memset(w2s_raw[:].bitcast(I32), 0)
         nc.gpsimd.memset(w4s[:].bitcast(I32), 0)
-        load_scale_rows(nc.gpsimd, w4s, w4_scales[0])
-        nc.gpsimd.dma_start(out=gain_sb[:], in_=gain.rearrange("(p t) -> p t", t=PACK))
 
         x_rows = xT.rearrange("(a p i) t -> a i p t", a=2, i=PACK)
         w1_rows = w1.rearrange("(a p i) r -> a p i r", a=2, i=PACK)
@@ -82,100 +79,83 @@ def tile_list_template_contact_gate_kernel(
             nc.sync.dma_start(out=planes[u][:], in_=x_rows[u // PACK, u % PACK])
 
         nc.sync.dma_start(offs_sb[:], offs)
+        nc.sync.dma_start(out=w2w_raw[:].bitcast(I32), in_=w2_words[0].bitcast(I32))
         nc.sync.dma_start(out=wgt_sb[:, :512], in_=wgt[:, :512])
-        load_scale_rows(nc.sync, tabs, tab_scales[0])
+        for q in range(4):
+            load_scale_quadrant(tabs, tab_scales[0], q)
         load_plane(0)
         nc.sync.dma_start(offs2_sb[:], offs2)
         nc.sync.dma_start(out=wgt_sb[:, 512:], in_=wgt[:, 512:])
-        for u in range(1, 4):
-            load_plane(u)
-        nc.sync.dma_start(out=w2w_raw[:].bitcast(I32), in_=w2_words[0].bitcast(I32))
-        load_scale_rows(nc.sync, w2s_raw, w2_scales[0])
+        load_plane(1)
+        load_scale_quadrant(w2s_raw, w2_scales[0], 0)
+        load_scale_quadrant(w2s_raw, w2_scales[0], 1)
+        load_plane(2)
+        load_scale_quadrant(w2s_raw, w2_scales[0], 2)
+        load_scale_quadrant(w2s_raw, w2_scales[0], 3)
+        load_plane(3)
+        nc.sync.dma_start(out=gain_sb[:], in_=gain.rearrange("(p t) -> p t", t=PACK))
         load_plane(4)
+        load_scale_quadrant(w4s, w4_scales[0], 0)
         load_plane(5)
+        load_scale_quadrant(w4s, w4_scales[0], 1)
         nc.sync.dma_start(out=w1_raw[0][:], in_=w1_rows[0])
+        load_scale_quadrant(w4s, w4_scales[0], 2)
         load_plane(6)
-        load_plane(7)
+        load_scale_quadrant(w4s, w4_scales[0], 3)
         nc.sync.dma_start(out=w1_raw[1][:], in_=w1_rows[1])
+        load_plane(7)
         nc.sync.dma_start(out=tabw[:].bitcast(I32), in_=tab_words[0].rearrange("p t i -> p (t i)").bitcast(I32))
-        for a in range(2):
-            nc.sync.dma_start(out=w3_raw[a][:], in_=w3_rows[a])
+        nc.sync.dma_start(out=w3_raw[0][:], in_=w3_rows[0])
+        nc.sync.dma_start(out=w3_raw[1][:], in_=w3_rows[1])
         nc.sync.dma_start(out=w4w[:].bitcast(I32), in_=w4_words[0].rearrange("p n i -> p (n i)").bitcast(I32))
 
         vs = held([P, S], U8, "vs")
-        vw = held([P, S], U32, "vw")
-        nc.vector.tensor_copy(vs[:], tabs[:].indirect(offs_sb[:]))
-
+        vw = {}
         g0 = held([P, PACK, S], F32, "g0")
+        g1 = held([P, PACK, S], F32, "g1")
         xq = [held([P, S], U32, f"xq{a}") for a in range(2)]
         w1q = [held([P, H], U32, f"w1q{a}") for a in range(2)]
-        w3q = [held([P, N], U32, f"w3q{a}") for a in range(2)]
-        w3s = [held([P, N], U8, f"w3s{a}") for a in range(2)]
+        w3q = held([P, 2 * N], U32, "w3q")
+        w3s = held([P, 2 * N], U8, "w3s")
         w1b = [held([P, PACK * H], BF16, f"w1b{a}") for a in range(2)]
-        w3b = [held([P, PACK * N], BF16, f"w3b{a}") for a in range(2)]
-        for h in range(2):
-            cols = slice(512 * h, 512 * (h + 1))
-            nc.vector.tensor_tensor(g0[:, 0, cols], planes[0][:].indirect(offs2_sb[:, 32 * h : 32 * (h + 1)]), wgt_sb[:, cols], MULT)
-        for i in range(1, PACK):
-            nc.vector.tensor_tensor(g0[:, i, :], planes[i][:].indirect(offs2_sb[:]), wgt_sb[:], MULT)
+        w3b = held([P, 2 * PACK * N], BF16, "w3b")
         xb0 = [held([P, PACK * 512], BF16, f"xb0_{h}") for h in range(2)]
-        for h in range(2):
-            interleave(nc.scalar.copy, xb0[h][:], g0[:, :, 512 * h : 512 * (h + 1)])
-        interleave_dealt(nc.scalar.copy, w1b[0][:], w1_raw[0][:])
-        chunks = S // CHUNK
-        g1 = held([P, PACK, S], F32, "g1")
-
-        def gather1(i, j, width):
-            lists = offs2_sb[:, j // 16 : (j + width) // 16]
-            nc.vector.tensor_tensor(g1[:, i, j : j + width], planes[PACK + i][:].indirect(lists), wgt_sb[:, j : j + width], MULT)
-
-        def quantize_w3(a):
-            quantize(w3q[a][:, :256], w3s[a][:, :256], w3b[a][:, :1024])
-            quantize(w3q[a][:, 256:], w3s[a][:, 256:], w3b[a][:, 1024:])
-
-        gather1(0, 0, S)
-        w2_both = held([P, 3 * H], U8, "w2_both", "plane4")
-        w2w = w2_both[:, : 2 * H]
-        w2s = w2_both[:, 2 * H :]
-        gather1(1, 0, S)
-        nc.vector.tensor_copy(
-            out=w2w.rearrange("p (t m b) -> p t m b", t=PACK, b=2),
-            in_=w2w_raw[:].rearrange("p (m t b) -> p t m b", t=PACK, b=2),
-        )
-        nc.vector.tensor_copy(out=w2s.rearrange("p (t m) -> p t m", t=PACK), in_=w2s_raw[:].rearrange("p (m t) -> p t m", t=PACK))
-        xs0 = held([P, S], U8, "xs0", "plane5")
-        for h in range(2):
-            quantize(xq[0][:, 512 * h : 512 * (h + 1)], xs0[:, 512 * h : 512 * (h + 1)], xb0[h][:])
-        gather1(2, 0, S)
-        for c in range(chunks):
-            gather1(PACK - 1, c * CHUNK, CHUNK)
-        w1s_both = held([P, 2 * H], U8, "w1s_both", "plane7")
-        w1s = [w1s_both[:, a * H : (a + 1) * H] for a in range(2)]
-        quantize(w1q[0][:], w1s[0], w1b[0][:])
-        interleave_dealt(nc.vector.tensor_copy, w1b[1][:], w1_raw[1][:])
         xs1 = held([P, S], U8, "xs1")
+        hq = held([P, S], U32, "hq")
+        hs = held([P, S], U8, "hs")
+        out_rows = out.rearrange("(m p) j -> p m j", p=P)
+        vector, scalar = nc.vector.tensor_copy, nc.scalar.copy
 
-        def xs(a, j, width):
-            return (xs0, xs1)[a][:, j : j + width]
+        def gather_x(u, j, width):
+            lists = offs2_sb[:, j // 16 : (j + width) // 16]
+            picked = (g0, g1)[u // PACK][:, u % PACK, j : j + width]
+            nc.vector.tensor_tensor(picked, planes[u][:].indirect(lists), wgt_sb[:, j : j + width], MULT)
 
-        for c in range(chunks):
-            j = c * CHUNK
-            cols = slice(j, j + CHUNK)
-            xb1 = ring.tile([P, PACK * CHUNK], BF16, name="xb1", align_bytes=64, bufs=4)
-            interleave(nc.scalar.copy, xb1[:], g1[:, :, cols])
-            quantize(xq[1][:, cols], xs1[:, cols], xb1[:])
-            if c == 0:
-                quantize(w1q[1][:], w1s[1], w1b[1][:])
-            nc.vector.tensor_copy(vw[:, cols], tabw[:].indirect(offs_sb[:, j // 16 : (j + CHUNK) // 16]))
-        interleave(nc.vector.tensor_copy, w3b[0][:], w3_raw[0][:])
-        interleave(nc.vector.tensor_copy, w3b[1][:], w3_raw[1][:])
-        for a in range(2):
-            quantize_w3(a)
+        def gather_words(j, width, tag=None):
+            words = held([P, width], U32, f"vw{j}", tag)
+            nc.vector.tensor_copy(words[:], tabw[:].indirect(offs_sb[:, j // 16 : (j + width) // 16]))
+            for s in range(0, width, SUB):
+                vw[j + s] = words[:, s : s + SUB]
+
+        def deal(dst, src):
+            nc.vector.tensor_copy(out=dst.rearrange("p (t m) -> p t m", t=PACK), in_=src.rearrange("p (m t) -> p t m", t=PACK))
+
+        def round_x1(copy, j, width, tag=None):
+            xb1 = held([P, PACK * width], BF16, f"xb1_{j}", tag)
+            interleave(copy, xb1[:], g1[:, :, j : j + width])
+            return xb1
+
+        def quantize_x1(xb1, j, width):
+            quantize(xq[1][:, j : j + width], xs1[:, j : j + width], xb1[:])
+
+        def round_w3(copy, a):
+            interleave(copy, w3b[:, a * PACK * N : (a + 1) * PACK * N], w3_raw[a][:])
+
+        def quantize_w3(j, width):
+            quantize(w3q[:, j : j + width], w3s[:, j : j + width], w3b[:, PACK * j : PACK * (j + width)])
 
         def mm(acc, lw, ls, rw, rs, start, stop):
             nc.tensor.matmul_mx(out=acc, lhsT=lw, lhsT_scale=ls, rhs=rw, rhs_scale=rs, start=start, stop=stop)
-
-        out_rows = out.rearrange("(m p) j -> p m j", p=P)
 
         def closeness(j0, width):
             absd = ring.tile([P, width * PACK], F32, name="absd")
@@ -185,17 +165,20 @@ def tile_list_template_contact_gate_kernel(
                 for a in range(2):
                     for t in range(PACK):
                         w = slice(t * P, (t + 1) * P)
-                        mm(d[:, t, :], w1q[a][:, w].bitcast(FP8X4), w1s[a][:, w], xq[a][:, cols].bitcast(FP8X4), xs(a, j0 + s * SUB, SUB), a == 0 and t == 0, False)
+                        mm(d[:, t, :], w1q[a][:, w].bitcast(FP8X4), w1s[a][:, w], xq[a][:, cols].bitcast(FP8X4), xs(a, cols), a == 0 and t == 0, False)
                 for t in range(PACK):
                     w = slice(t * P, (t + 1) * P)
-                    mm(d[:, t, :], w2w[:, 2 * t * P : 2 * (t + 1) * P].bitcast(FP4X4), w2s[:, w], vw[:, cols].bitcast(FP8X4), vs[:, cols], False, t == PACK - 1)
+                    mm(d[:, t, :], w2w[:, 2 * t * P : 2 * (t + 1) * P].bitcast(FP4X4), w2s[:, w], vw[cols.start].bitcast(FP8X4), vs[:, cols], False, t == PACK - 1)
                 nc.scalar.activation(
                     out=absd[:, s * SUB * PACK : (s + 1) * SUB * PACK].rearrange("p (j t) -> p j t", t=PACK),
                     in_=d[:].rearrange("p t j -> p j t"),
                     func=ACT.Abs,
                 )
-            e = ring.tile([P, width * PACK], F32, name="e")
+            e = ring.tile([P, width * PACK], F32, name="e", bufs=3)
             nc.scalar.activation(out=e[:], in_=absd[:], func=ACT.Exp, scale=-1.0)
+            return e
+
+        def apply_gain(e, width):
             hb = ring.tile([P, width * PACK], BF16, name="hb", align_bytes=64)
             nc.vector.tensor_tensor(
                 hb[:].rearrange("p (j t) -> p j t", t=PACK),
@@ -203,34 +186,81 @@ def tile_list_template_contact_gate_kernel(
                 gain_sb[:].unsqueeze(1).to_broadcast([P, width, PACK]),
                 MULT,
             )
-            hq = ring.tile([P, width], U32, name="hq", align_bytes=64)
-            hs = ring.tile([P, width], U8, name="hs", align_bytes=64)
-            quantize(hq[:], hs[:], hb[:])
-            return hq, hs
+            return hb
 
-        def finish(j0, width, hq, hs):
+        def quantize_h(hb, j, width):
+            quantize(hq[:, j : j + width], hs[:, j : j + width], hb[:])
+
+        def project(copy, j):
+            cols = slice(j, j + SUB)
+            r = psum.tile([P, N_TILES, SUB], F32, name="r", bufs=2)
+            for m in range(N_TILES):
+                for a in range(2):
+                    w = slice(a * N + m * P, a * N + (m + 1) * P)
+                    mm(r[:, m, :], w3q[:, w].bitcast(FP8X4), w3s[:, w], xq[a][:, cols].bitcast(FP8X4), xs(a, cols), a == 0, a == 1)
+            r_sb = r_all[j // 512][:, j % 512 // SUB]
+            copy(out=r_sb, in_=r[:])
+            return r_sb
+
+        def finish(j0, width, projected):
             ob = ring.tile([P, N_TILES, width], F32, name="ob", bufs=3)
             for s in range(width // SUB):
                 cols = slice(j0 + s * SUB, j0 + (s + 1) * SUB)
-                sub = slice(s * SUB, (s + 1) * SUB)
-                r = psum.tile([P, N_TILES, SUB], F32, name="r", bufs=2)
-                for m in range(N_TILES):
-                    w = slice(m * P, (m + 1) * P)
-                    for a in range(2):
-                        mm(r[:, m, :], w3q[a][:, w].bitcast(FP8X4), w3s[a][:, w], xq[a][:, cols].bitcast(FP8X4), xs(a, j0 + s * SUB, SUB), a == 0, a == 1)
-                r_sb = ring.tile([P, N_TILES, SUB], F32, name="r_sb", bufs=4)
-                nc.scalar.copy(out=r_sb[:], in_=r[:])
                 y = psum.tile([P, N_TILES, SUB], F32, name="y", bufs=2)
                 for m in range(N_TILES):
                     w = slice(m * P, (m + 1) * P)
-                    mm(y[:, m, :], w4w[:, w].bitcast(FP8X4), w4s[:, w], hq[:, sub].bitcast(FP8X4), hs[:, sub], True, True)
-                nc.vector.tensor_tensor(ob[:, :, sub], y[:], r_sb[:], MULT)
+                    mm(y[:, m, :], w4w[:, w].bitcast(FP8X4), w4s[:, w], hq[:, cols].bitcast(FP8X4), hs[:, cols], True, True)
+                nc.vector.tensor_tensor(ob[:, :, s * SUB : (s + 1) * SUB], y[:], projected[s], MULT)
             nc.sync.dma_start(out=out_rows[:, :, j0 : j0 + width], in_=ob[:])
 
+        w2w = held([P, 2 * H], U8, "w2w")
+        deal(w2w[:].bitcast(U16), w2w_raw[:].bitcast(U16))
+        nc.vector.tensor_copy(vs[:], tabs[:].indirect(offs_sb[:]))
+        for h in range(2):
+            gather_x(0, 512 * h, 512)
+        for u in range(1, PACK):
+            gather_x(u, 0, S)
+        r_all = [held([P, 512 // SUB, N_TILES, SUB], F32, f"r_all{h}", f"plane{h}") for h in range(2)]
+        for h in range(2):
+            interleave(scalar, xb0[h][:], g0[:, :, 512 * h : 512 * (h + 1)])
+        for a in range(2):
+            interleave_dealt(scalar, w1b[a][:], w1_raw[a][:])
+        gather_x(4, 0, S)
+        gather_x(5, 0, S)
+        early = held([P, H + S], U8, "early", "plane5")
+        w2s = early[:, :H]
+        deal(w2s, w2s_raw[:])
+        for h in range(2):
+            quantize(xq[0][:, 512 * h : 512 * (h + 1)], early[:, H + 512 * h : H + 512 * (h + 1)], xb0[h][:])
+        gather_x(6, 0, S)
+        w1s = [held([P, H], U8, "w1s0", "plane6")[:]]
+        quantize(w1q[0][:], w1s[0], w1b[0][:])
+
+        def xs(a, cols):
+            if a == 1:
+                return xs1[:, cols]
+            return early[:, H + cols.start : H + cols.stop]
+
+        gather_x(7, 0, CHUNK)
+        gather_x(7, CHUNK, CHUNK)
+        gather_x(7, 512, 512)
+        w1s.append(held([P, H], U8, "w1s1", "plane7")[:])
+        quantize(w1q[1][:], w1s[1], w1b[1][:])
+        quantize_x1(round_x1(scalar, 0, CHUNK), 0, CHUNK)
+        gather_words(0, CHUNK)
+        quantize_x1(round_x1(scalar, CHUNK, CHUNK), CHUNK, CHUNK)
+        gather_words(CHUNK, CHUNK, "xb1_0")
+        gather_words(512, 512)
+        quantize_x1(round_x1(scalar, 512, 512), 512, 512)
+        for a in range(2):
+            round_w3(vector, a)
+        quantize_w3(0, 256)
+        quantize_w3(256, 512)
         groups = [(0, 256), (256, 256), (512, 256), (768, 128), (896, 128)]
-        made = []
-        for g in range(len(groups) + 1):
-            if g < len(groups):
-                made.append(closeness(*groups[g]))
-            if g >= 1:
-                finish(*groups[g - 1], *made[g - 1])
+        for g, (j, width) in enumerate(groups):
+            quantize_h(apply_gain(closeness(j, width), width), j, width)
+            if g in (1, 2):
+                j, width = groups[g - 1]
+                finish(j, width, [project(scalar, s) for s in range(j, j + width, SUB)])
+        for j, width in groups[2:]:
+            finish(j, width, [project(scalar, s) for s in range(j, j + width, SUB)])

@@ -1,6 +1,7 @@
 from contextlib import ExitStack
 
 import concourse.mybir as mybir
+from concourse.masks import make_identity
 
 K, C, T, S, H, N = 1024, 512, 2048, 1024, 512, 384
 FLOPS = 2 * S * (K * H + C * H + K * N + H * N)
@@ -18,6 +19,7 @@ ACT = mybir.ActivationFunctionType
 
 P = 128
 PACK = 4
+HALF = S // 2
 CHUNK = 256
 SUB = 128
 N_TILES = N // P
@@ -31,15 +33,19 @@ def tile_list_template_contact_gate_kernel(
         keep = ctx.enter_context(tc.tile_pool(name="keep", bufs=1))
         ring = ctx.enter_context(tc.tile_pool(name="ring", bufs=2))
         psum = ctx.enter_context(tc.psum_pool(name="psum", bufs=1))
+        on_vector, on_scalar = nc.vector.tensor_copy, nc.scalar.copy
 
         def held(shape, dtype, name, tag=None):
             return keep.tile(shape, dtype, name=name, tag=tag or name, align_bytes=64)
 
+        def load_words(tile, rows):
+            nc.sync.dma_start(out=tile.bitcast(I32), in_=rows.bitcast(I32))
+
+        def load_scale_rows(plane, rows, q):
+            load_words(plane[32 * q : 32 * q + 4, :], rows[4 * q : 4 * q + 4, :])
+
         def quantize(codes, scales, values):
             nc.vector.quantize_mx(out=codes.bitcast(FP8X4), scales=scales, in_=values)
-
-        def load_scale_quadrant(plane, rows, q):
-            nc.sync.dma_start(out=plane[32 * q : 32 * q + 4, :].bitcast(I32), in_=rows[4 * q : 4 * q + 4, :].bitcast(I32))
 
         def interleave(copy, dst, src):
             copy(
@@ -53,23 +59,35 @@ def tile_list_template_contact_gate_kernel(
                 in_=src.rearrange("p i (m t) -> p m i t", t=PACK),
             )
 
+        def deal(dst, src):
+            on_vector(out=dst.rearrange("p (t m) -> p t m", t=PACK), in_=src.rearrange("p (m t) -> p t m", t=PACK))
+
+        def mm(acc, lhs, rhs, start, stop):
+            nc.tensor.matmul_mx(out=acc, lhsT=lhs[0], lhsT_scale=lhs[1], rhs=rhs[0], rhs_scale=rhs[1], start=start, stop=stop)
+
         offs_sb = held([P, S // 16], U16, "offs_sb")
         offs2_sb = held([P, S // 16], U16, "offs2_sb")
         tabw = held([P, T], U32, "tabw")
         tabs = held([P, T], U8, "tabs")
+        wgt_rows = held([P, P], F32, "wgt_rows")
         wgt_sb = held([P, S], F32, "wgt_sb")
         planes = [held([P, T], F32, f"plane{u}") for u in range(8)]
         w1_raw = [held([P, PACK, H], F32, f"w1_raw{a}") for a in range(2)]
         w3_raw = [held([P, PACK, N], F32, f"w3_raw{a}") for a in range(2)]
         w2w_raw = held([P, 2 * H], U8, "w2w_raw")
         w2s_raw = held([P, H], U8, "w2s_raw")
+        w2w = held([P, 2 * H], U8, "w2w")
         w4w = held([P, N], U32, "w4w")
         w4s = held([P, N], U8, "w4s")
         gain_sb = held([P, PACK], F32, "gain_sb")
+        ident = held([P, P], F32, "ident")
+        vs_rows = held([P, S], U8, "vs_rows")
+        vs = held([P, S], U8, "vs")
 
         nc.gpsimd.memset(tabs[:].bitcast(I32), 0)
-        nc.gpsimd.memset(w2s_raw[:].bitcast(I32), 0)
-        nc.gpsimd.memset(w4s[:].bitcast(I32), 0)
+        make_identity(nc, ident[:])
+        for plane in (w2s_raw, w4s, vs):
+            nc.gpsimd.memset(plane[:].bitcast(I32), 0)
 
         x_rows = xT.rearrange("(a p i) t -> a i p t", a=2, i=PACK)
         w1_rows = w1.rearrange("(a p i) r -> a p i r", a=2, i=PACK)
@@ -78,84 +96,93 @@ def tile_list_template_contact_gate_kernel(
         def load_plane(u):
             nc.sync.dma_start(out=planes[u][:], in_=x_rows[u // PACK, u % PACK])
 
+        nc.sync.dma_start(out=wgt_rows[:], in_=wgt.rearrange("(g r) (b j) -> g (r b) j", r=16, j=P)[:, :16, :])
+        load_words(w2w_raw[:], w2_words[0])
         nc.sync.dma_start(offs_sb[:], offs)
-        nc.sync.dma_start(out=w2w_raw[:].bitcast(I32), in_=w2_words[0].bitcast(I32))
-        nc.sync.dma_start(out=wgt_sb[:, :512], in_=wgt[:, :512])
-        for q in range(4):
-            load_scale_quadrant(tabs, tab_scales[0], q)
+        load_words(tabs[:16, :], tab_scales[0])
         load_plane(0)
+        deal(w2w[:].bitcast(U16), w2w_raw[:].bitcast(U16))
+        on_vector(vs_rows[:], tabs[:].indirect(offs_sb[:]))
         nc.sync.dma_start(offs2_sb[:], offs2)
-        nc.sync.dma_start(out=wgt_sb[:, 512:], in_=wgt[:, 512:])
         load_plane(1)
-        load_scale_quadrant(w2s_raw, w2_scales[0], 0)
-        load_scale_quadrant(w2s_raw, w2_scales[0], 1)
+        load_scale_rows(w2s_raw, w2_scales[0], 0)
+        load_scale_rows(w2s_raw, w2_scales[0], 1)
         load_plane(2)
-        load_scale_quadrant(w2s_raw, w2_scales[0], 2)
-        load_scale_quadrant(w2s_raw, w2_scales[0], 3)
+        load_scale_rows(w2s_raw, w2_scales[0], 2)
+        load_scale_rows(w2s_raw, w2_scales[0], 3)
         load_plane(3)
+        load_scale_rows(vs, vs_rows, 0)
+        load_scale_rows(vs, vs_rows, 1)
+        load_scale_rows(vs, vs_rows, 2)
+        load_scale_rows(vs, vs_rows, 3)
         nc.sync.dma_start(out=gain_sb[:], in_=gain.rearrange("(p t) -> p t", t=PACK))
         load_plane(4)
-        load_scale_quadrant(w4s, w4_scales[0], 0)
+        load_scale_rows(w4s, w4_scales[0], 0)
         load_plane(5)
-        load_scale_quadrant(w4s, w4_scales[0], 1)
+        load_scale_rows(w4s, w4_scales[0], 1)
         nc.sync.dma_start(out=w1_raw[0][:], in_=w1_rows[0])
-        load_scale_quadrant(w4s, w4_scales[0], 2)
+        load_scale_rows(w4s, w4_scales[0], 2)
         load_plane(6)
-        load_scale_quadrant(w4s, w4_scales[0], 3)
+        load_scale_rows(w4s, w4_scales[0], 3)
         nc.sync.dma_start(out=w1_raw[1][:], in_=w1_rows[1])
         load_plane(7)
-        nc.sync.dma_start(out=tabw[:].bitcast(I32), in_=tab_words[0].rearrange("p t i -> p (t i)").bitcast(I32))
+        load_words(tabw[:], tab_words[0].rearrange("p t i -> p (t i)"))
         nc.sync.dma_start(out=w3_raw[0][:], in_=w3_rows[0])
         nc.sync.dma_start(out=w3_raw[1][:], in_=w3_rows[1])
-        nc.sync.dma_start(out=w4w[:].bitcast(I32), in_=w4_words[0].rearrange("p n i -> p (n i)").bitcast(I32))
+        load_words(w4w[:], w4_words[0].rearrange("p n i -> p (n i)"))
 
-        vs = held([P, S], U8, "vs")
-        vw = {}
-        g0 = held([P, PACK, S], F32, "g0")
-        g1 = held([P, PACK, S], F32, "g1")
+        turned = psum.tile([P, P], F32, name="turned", tag="y", bufs=2)
+        nc.tensor.transpose(turned[:], wgt_rows[:], ident[:])
+        for h in range(2):
+            spread = held([P, 4, P], F32, f"spread{h}")
+            on_scalar(
+                out=spread[:].rearrange("j b (q e) -> j b q e", e=8),
+                in_=turned[:].rearrange("j (q b) -> j b q", b=8)[:, 4 * h : 4 * h + 4, :].unsqueeze(3).to_broadcast([P, 4, 16, 8]),
+            )
+            back = psum.tile([P, 4, P], F32, name="back", tag="r", bufs=2)
+            for b in range(4):
+                nc.tensor.transpose(back[:, b, :], spread[:, b, :], ident[:])
+            on_scalar(out=wgt_sb[:, HALF * h : HALF * (h + 1)], in_=back[:].rearrange("p b j -> p (b j)"))
+
+        picked = [held([P, PACK, S], F32, f"picked{a}") for a in range(2)]
         xq = [held([P, S], U32, f"xq{a}") for a in range(2)]
         w1q = [held([P, H], U32, f"w1q{a}") for a in range(2)]
+        w1b = [held([P, PACK * H], BF16, f"w1b{a}") for a in range(2)]
         w3q = held([P, 2 * N], U32, "w3q")
         w3s = held([P, 2 * N], U8, "w3s")
-        w1b = [held([P, PACK * H], BF16, f"w1b{a}") for a in range(2)]
-        w3b = held([P, 2 * PACK * N], BF16, "w3b")
-        xb0 = [held([P, PACK * 512], BF16, f"xb0_{h}") for h in range(2)]
         xs1 = held([P, S], U8, "xs1")
         hq = held([P, S], U32, "hq")
         hs = held([P, S], U8, "hs")
+        vw = {}
         out_rows = out.rearrange("(m p) j -> p m j", p=P)
-        vector, scalar = nc.vector.tensor_copy, nc.scalar.copy
 
         def gather_x(u, j, width):
             lists = offs2_sb[:, j // 16 : (j + width) // 16]
-            picked = (g0, g1)[u // PACK][:, u % PACK, j : j + width]
-            nc.vector.tensor_tensor(picked, planes[u][:].indirect(lists), wgt_sb[:, j : j + width], MULT)
+            dst = picked[u // PACK][:, u % PACK, j : j + width]
+            nc.vector.tensor_tensor(dst, planes[u][:].indirect(lists), wgt_sb[:, j : j + width], MULT)
 
         def gather_words(j, width, tag=None):
             words = held([P, width], U32, f"vw{j}", tag)
-            nc.vector.tensor_copy(words[:], tabw[:].indirect(offs_sb[:, j // 16 : (j + width) // 16]))
+            on_vector(words[:], tabw[:].indirect(offs_sb[:, j // 16 : (j + width) // 16]))
             for s in range(0, width, SUB):
                 vw[j + s] = words[:, s : s + SUB]
 
-        def deal(dst, src):
-            nc.vector.tensor_copy(out=dst.rearrange("p (t m) -> p t m", t=PACK), in_=src.rearrange("p (m t) -> p t m", t=PACK))
+        def round_x(copy, a, j, width, tag=None):
+            rounded = held([P, PACK * width], BF16, f"xb{a}_{j}", tag)
+            interleave(copy, rounded[:], picked[a][:, :, j : j + width])
+            return rounded
 
-        def round_x1(copy, j, width, tag=None):
-            xb1 = held([P, PACK * width], BF16, f"xb1_{j}", tag)
-            interleave(copy, xb1[:], g1[:, :, j : j + width])
-            return xb1
+        def quantize_x(a, j, width, rounded):
+            quantize(xq[a][:, j : j + width], xs[a][:, j : j + width], rounded[:])
 
-        def quantize_x1(xb1, j, width):
-            quantize(xq[1][:, j : j + width], xs1[:, j : j + width], xb1[:])
-
-        def round_w3(copy, a):
-            interleave(copy, w3b[:, a * PACK * N : (a + 1) * PACK * N], w3_raw[a][:])
+        def round_w3(copy, a, c0=0, c1=N):
+            interleave(copy, w3b[:, PACK * (a * N + c0) : PACK * (a * N + c1)], w3_raw[a][:, :, c0:c1])
 
         def quantize_w3(j, width):
             quantize(w3q[:, j : j + width], w3s[:, j : j + width], w3b[:, PACK * j : PACK * (j + width)])
 
-        def mm(acc, lw, ls, rw, rs, start, stop):
-            nc.tensor.matmul_mx(out=acc, lhsT=lw, lhsT_scale=ls, rhs=rw, rhs_scale=rs, start=start, stop=stop)
+        def x_operand(a, cols):
+            return xq[a][:, cols].bitcast(FP8X4), xs[a][:, cols]
 
         def closeness(j0, width):
             absd = ring.tile([P, width * PACK], F32, name="absd")
@@ -165,10 +192,10 @@ def tile_list_template_contact_gate_kernel(
                 for a in range(2):
                     for t in range(PACK):
                         w = slice(t * P, (t + 1) * P)
-                        mm(d[:, t, :], w1q[a][:, w].bitcast(FP8X4), w1s[a][:, w], xq[a][:, cols].bitcast(FP8X4), xs(a, cols), a == 0 and t == 0, False)
+                        mm(d[:, t, :], (w1q[a][:, w].bitcast(FP8X4), w1s[a][:, w]), x_operand(a, cols), a == 0 and t == 0, False)
                 for t in range(PACK):
-                    w = slice(t * P, (t + 1) * P)
-                    mm(d[:, t, :], w2w[:, 2 * t * P : 2 * (t + 1) * P].bitcast(FP4X4), w2s[:, w], vw[cols.start].bitcast(FP8X4), vs[:, cols], False, t == PACK - 1)
+                    lhs = w2w[:, 2 * t * P : 2 * (t + 1) * P].bitcast(FP4X4), w2s[:, t * P : (t + 1) * P]
+                    mm(d[:, t, :], lhs, (vw[cols.start].bitcast(FP8X4), vs[:, cols]), False, t == PACK - 1)
                 nc.scalar.activation(
                     out=absd[:, s * SUB * PACK : (s + 1) * SUB * PACK].rearrange("p (j t) -> p j t", t=PACK),
                     in_=d[:].rearrange("p t j -> p j t"),
@@ -197,70 +224,62 @@ def tile_list_template_contact_gate_kernel(
             for m in range(N_TILES):
                 for a in range(2):
                     w = slice(a * N + m * P, a * N + (m + 1) * P)
-                    mm(r[:, m, :], w3q[:, w].bitcast(FP8X4), w3s[:, w], xq[a][:, cols].bitcast(FP8X4), xs(a, cols), a == 0, a == 1)
-            r_sb = r_all[j // 512][:, j % 512 // SUB]
+                    mm(r[:, m, :], (w3q[:, w].bitcast(FP8X4), w3s[:, w]), x_operand(a, cols), a == 0, a == 1)
+            r_sb = r_all[j // HALF][:, j % HALF // SUB]
             copy(out=r_sb, in_=r[:])
             return r_sb
 
-        def finish(j0, width, projected):
+        def finish(j0, width, copy=on_scalar):
+            projected = [project(copy, j) for j in range(j0, j0 + width, SUB)]
             ob = ring.tile([P, N_TILES, width], F32, name="ob", bufs=3)
             for s in range(width // SUB):
                 cols = slice(j0 + s * SUB, j0 + (s + 1) * SUB)
                 y = psum.tile([P, N_TILES, SUB], F32, name="y", bufs=2)
                 for m in range(N_TILES):
                     w = slice(m * P, (m + 1) * P)
-                    mm(y[:, m, :], w4w[:, w].bitcast(FP8X4), w4s[:, w], hq[:, cols].bitcast(FP8X4), hs[:, cols], True, True)
+                    mm(y[:, m, :], (w4w[:, w].bitcast(FP8X4), w4s[:, w]), (hq[:, cols].bitcast(FP8X4), hs[:, cols]), True, True)
                 nc.vector.tensor_tensor(ob[:, :, s * SUB : (s + 1) * SUB], y[:], projected[s], MULT)
             nc.sync.dma_start(out=out_rows[:, :, j0 : j0 + width], in_=ob[:])
 
-        w2w = held([P, 2 * H], U8, "w2w")
-        deal(w2w[:].bitcast(U16), w2w_raw[:].bitcast(U16))
-        nc.vector.tensor_copy(vs[:], tabs[:].indirect(offs_sb[:]))
         for h in range(2):
-            gather_x(0, 512 * h, 512)
+            gather_x(0, HALF * h, HALF)
         for u in range(1, PACK):
             gather_x(u, 0, S)
-        r_all = [held([P, 512 // SUB, N_TILES, SUB], F32, f"r_all{h}", f"plane{h}") for h in range(2)]
-        for h in range(2):
-            interleave(scalar, xb0[h][:], g0[:, :, 512 * h : 512 * (h + 1)])
+        r_all = [held([P, HALF // SUB, N_TILES, SUB], F32, f"r_all{h}", f"plane{h}") for h in range(2)]
+        w3b = held([P, 2 * PACK * N], BF16, "w3b", "plane2")
+        xb0 = [round_x(on_scalar, 0, HALF * h, HALF) for h in range(2)]
         for a in range(2):
-            interleave_dealt(scalar, w1b[a][:], w1_raw[a][:])
+            interleave_dealt(on_scalar, w1b[a][:], w1_raw[a][:])
         gather_x(4, 0, S)
         gather_x(5, 0, S)
-        early = held([P, H + S], U8, "early", "plane5")
-        w2s = early[:, :H]
+        behind5 = held([P, H + S], U8, "behind5", "plane5")
+        w2s = behind5[:, :H]
+        xs = (behind5[:, H:], xs1)
         deal(w2s, w2s_raw[:])
         for h in range(2):
-            quantize(xq[0][:, 512 * h : 512 * (h + 1)], early[:, H + 512 * h : H + 512 * (h + 1)], xb0[h][:])
+            quantize_x(0, HALF * h, HALF, xb0[h])
         gather_x(6, 0, S)
-        w1s = [held([P, H], U8, "w1s0", "plane6")[:]]
-        quantize(w1q[0][:], w1s[0], w1b[0][:])
-
-        def xs(a, cols):
-            if a == 1:
-                return xs1[:, cols]
-            return early[:, H + cols.start : H + cols.stop]
-
+        w1s = [held([P, H], U8, "w1s0", "plane6")]
+        quantize(w1q[0][:], w1s[0][:], w1b[0][:])
         gather_x(7, 0, CHUNK)
         gather_x(7, CHUNK, CHUNK)
-        gather_x(7, 512, 512)
-        w1s.append(held([P, H], U8, "w1s1", "plane7")[:])
-        quantize(w1q[1][:], w1s[1], w1b[1][:])
-        quantize_x1(round_x1(scalar, 0, CHUNK), 0, CHUNK)
+        gather_x(7, HALF, HALF)
+        w1s.append(held([P, H], U8, "w1s1", "plane7"))
+        quantize(w1q[1][:], w1s[1][:], w1b[1][:])
+        quantize_x(1, 0, CHUNK, round_x(on_scalar, 1, 0, CHUNK))
         gather_words(0, CHUNK)
-        quantize_x1(round_x1(scalar, CHUNK, CHUNK), CHUNK, CHUNK)
+        quantize_x(1, CHUNK, CHUNK, round_x(on_scalar, 1, CHUNK, CHUNK))
         gather_words(CHUNK, CHUNK, "xb1_0")
-        gather_words(512, 512)
-        quantize_x1(round_x1(scalar, 512, 512), 512, 512)
+        gather_words(HALF, HALF)
+        quantize_x(1, HALF, HALF, round_x(on_scalar, 1, HALF, HALF))
         for a in range(2):
-            round_w3(vector, a)
+            round_w3(on_vector, a)
         quantize_w3(0, 256)
         quantize_w3(256, 512)
         groups = [(0, 256), (256, 256), (512, 256), (768, 128), (896, 128)]
         for g, (j, width) in enumerate(groups):
             quantize_h(apply_gain(closeness(j, width), width), j, width)
             if g in (1, 2):
-                j, width = groups[g - 1]
-                finish(j, width, [project(scalar, s) for s in range(j, j + width, SUB)])
+                finish(*groups[g - 1])
         for j, width in groups[2:]:
-            finish(j, width, [project(scalar, s) for s in range(j, j + width, SUB)])
+            finish(j, width)

@@ -73,7 +73,7 @@ def tile_list_template_contact_gate_kernel(
         wgt_sb = held([P, S], F32, "wgt_sb")
         planes = [held([P, T], F32, f"plane{u}") for u in range(8)]
         w1_raw = [held([P, PACK, H], F32, f"w1_raw{a}") for a in range(2)]
-        w3_raw = [held([P, PACK, N], F32, f"w3_raw{a}") for a in range(2)]
+        w3_raw = held([P, 2, PACK, N], F32, "w3_raw")
         w2w_raw = held([P, 2 * H], U8, "w2w_raw")
         w2s_raw = held([P, H], U8, "w2s_raw")
         w2w = held([P, 2 * H], U8, "w2w")
@@ -111,10 +111,6 @@ def tile_list_template_contact_gate_kernel(
         load_scale_rows(w2s_raw, w2_scales[0], 2)
         load_scale_rows(w2s_raw, w2_scales[0], 3)
         load_plane(3)
-        load_scale_rows(vs, vs_rows, 0)
-        load_scale_rows(vs, vs_rows, 1)
-        load_scale_rows(vs, vs_rows, 2)
-        load_scale_rows(vs, vs_rows, 3)
         nc.sync.dma_start(out=gain_sb[:], in_=gain.rearrange("(p t) -> p t", t=PACK))
         load_plane(4)
         load_scale_rows(w4s, w4_scales[0], 0)
@@ -127,8 +123,12 @@ def tile_list_template_contact_gate_kernel(
         nc.sync.dma_start(out=w1_raw[1][:], in_=w1_rows[1])
         load_plane(7)
         load_words(tabw[:], tab_words[0].rearrange("p t i -> p (t i)"))
-        nc.sync.dma_start(out=w3_raw[0][:], in_=w3_rows[0])
-        nc.sync.dma_start(out=w3_raw[1][:], in_=w3_rows[1])
+        nc.sync.dma_start(out=w3_raw[:, 0], in_=w3_rows[0])
+        load_scale_rows(vs, vs_rows, 0)
+        load_scale_rows(vs, vs_rows, 1)
+        load_scale_rows(vs, vs_rows, 2)
+        load_scale_rows(vs, vs_rows, 3)
+        nc.sync.dma_start(out=w3_raw[:, 1], in_=w3_rows[1])
         load_words(w4w[:], w4_words[0].rearrange("p n i -> p (n i)"))
 
         turned = psum.tile([P, P], F32, name="turned", tag="y", bufs=2)
@@ -172,11 +172,20 @@ def tile_list_template_contact_gate_kernel(
             interleave(copy, rounded[:], picked[a][:, :, j : j + width])
             return rounded
 
+        def round_pair(copy, rounded, a, u, j, width):
+            copy(
+                out=rounded[:].rearrange("p (c i) -> p c i", i=PACK)[:, :, 2 * u : 2 * u + 2],
+                in_=picked[a][:, 2 * u : 2 * u + 2, j : j + width].rearrange("p i c -> p c i"),
+            )
+
         def quantize_x(a, j, width, rounded):
             quantize(xq[a][:, j : j + width], xs[a][:, j : j + width], rounded[:])
 
-        def round_w3(copy, a, c0=0, c1=N):
-            interleave(copy, w3b[:, PACK * (a * N + c0) : PACK * (a * N + c1)], w3_raw[a][:, :, c0:c1])
+        def round_w3(c0, c1):
+            on_vector(
+                out=w3b[:, 2 * PACK * c0 : 2 * PACK * c1].rearrange("p (a c e i) -> p a c i e", a=2, e=4, i=PACK),
+                in_=w3_raw[:, :, :, c0:c1].rearrange("p a i (c e) -> p a c i e", e=4),
+            )
 
         def quantize_w3(j, width):
             quantize(w3q[:, j : j + width], w3s[:, j : j + width], w3b[:, PACK * j : PACK * (j + width)])
@@ -205,8 +214,11 @@ def tile_list_template_contact_gate_kernel(
             nc.scalar.activation(out=e[:], in_=absd[:], func=ACT.Exp, scale=-1.0)
             return e
 
-        def apply_gain(e, width):
-            hb = ring.tile([P, width * PACK], BF16, name="hb", align_bytes=64)
+        def apply_gain(e, width, tag=None):
+            if tag:
+                hb = held([P, width * PACK], BF16, "hb_first", tag)
+            else:
+                hb = ring.tile([P, width * PACK], BF16, name="hb", align_bytes=64)
             nc.vector.tensor_tensor(
                 hb[:].rearrange("p (j t) -> p j t", t=PACK),
                 e[:].rearrange("p (j t) -> p j t", t=PACK),
@@ -220,10 +232,14 @@ def tile_list_template_contact_gate_kernel(
 
         def project(copy, j):
             cols = slice(j, j + SUB)
-            r = psum.tile([P, N_TILES, SUB], F32, name="r", bufs=2)
+            if j < HALF:
+                r = psum.tile([P, N_TILES, SUB], F32, name="r", bufs=2)
+            else:
+                r = psum.tile([P, N_TILES, SUB], F32, name="r", tag="d", bufs=4)
             for m in range(N_TILES):
                 for a in range(2):
-                    w = slice(a * N + m * P, a * N + (m + 1) * P)
+                    first = 256 * a + P * m if m < 2 else 512 + P * a
+                    w = slice(first, first + P)
                     mm(r[:, m, :], (w3q[:, w].bitcast(FP8X4), w3s[:, w]), x_operand(a, cols), a == 0, a == 1)
             r_sb = r_all[j // HALF][:, j % HALF // SUB]
             copy(out=r_sb, in_=r[:])
@@ -247,11 +263,19 @@ def tile_list_template_contact_gate_kernel(
             gather_x(u, 0, S)
         r_all = [held([P, HALF // SUB, N_TILES, SUB], F32, f"r_all{h}", f"plane{h}") for h in range(2)]
         w3b = held([P, 2 * PACK * N], BF16, "w3b", "plane2")
-        xb0 = [round_x(on_scalar, 0, HALF * h, HALF) for h in range(2)]
-        for a in range(2):
-            interleave_dealt(on_scalar, w1b[a][:], w1_raw[a][:])
+        xb0 = [held([P, PACK * HALF], BF16, f"xb0_{h}") for h in range(2)]
+        for u in range(2):
+            for h in range(2):
+                round_pair(on_scalar, xb0[h], 0, u, HALF * h, HALF)
+        interleave_dealt(on_scalar, w1b[0][:], w1_raw[0][:])
         gather_x(4, 0, S)
         gather_x(5, 0, S)
+        cuts = [(0, CHUNK), (CHUNK, CHUNK), (HALF, HALF)]
+        xb1_all = held([P, PACK * S], BF16, "xb1", "w1_raw0")
+        xb1 = [xb1_all[:, PACK * j : PACK * (j + width)] for j, width in cuts]
+        for rounded, (j, width) in zip(xb1, cuts):
+            round_pair(on_scalar, rounded, 1, 0, j, width)
+        interleave_dealt(on_scalar, w1b[1][:], w1_raw[1][:])
         behind5 = held([P, H + S], U8, "behind5", "plane5")
         w2s = behind5[:, :H]
         xs = (behind5[:, H:], xs1)
@@ -261,25 +285,29 @@ def tile_list_template_contact_gate_kernel(
         gather_x(6, 0, S)
         w1s = [held([P, H], U8, "w1s0", "plane6")]
         quantize(w1q[0][:], w1s[0][:], w1b[0][:])
-        gather_x(7, 0, CHUNK)
-        gather_x(7, CHUNK, CHUNK)
-        gather_x(7, HALF, HALF)
+        for rounded, (j, width) in zip(xb1, cuts):
+            gather_x(7, j, width)
+            round_pair(on_scalar, rounded, 1, 1, j, width)
         w1s.append(held([P, H], U8, "w1s1", "plane7"))
         quantize(w1q[1][:], w1s[1][:], w1b[1][:])
-        quantize_x(1, 0, CHUNK, round_x(on_scalar, 1, 0, CHUNK))
+        quantize_x(1, 0, CHUNK, xb1[0])
         gather_words(0, CHUNK)
-        quantize_x(1, CHUNK, CHUNK, round_x(on_scalar, 1, CHUNK, CHUNK))
-        gather_words(CHUNK, CHUNK, "xb1_0")
+        quantize_x(1, CHUNK, CHUNK, xb1[1])
+        gather_words(CHUNK, CHUNK, "w1b1")
         gather_words(HALF, HALF)
-        quantize_x(1, HALF, HALF, round_x(on_scalar, 1, HALF, HALF))
-        for a in range(2):
-            round_w3(on_vector, a)
-        quantize_w3(0, 256)
-        quantize_w3(256, 512)
-        groups = [(0, 256), (256, 256), (512, 256), (768, 128), (896, 128)]
-        for g, (j, width) in enumerate(groups):
-            quantize_h(apply_gain(closeness(j, width), width), j, width)
-            if g in (1, 2):
-                finish(*groups[g - 1])
-        for j, width in groups[2:]:
-            finish(j, width)
+        quantize_x(1, HALF, HALF, xb1[2])
+        round_w3(0, 256)
+        round_w3(256, N)
+        quantize_w3(0, 512)
+        hb = apply_gain(closeness(0, 256), 256, "w3_raw")
+        quantize_w3(512, 256)
+        quantize_h(hb, 0, 256)
+        quantize_h(apply_gain(closeness(256, 256), 256), 256, 256)
+        finish(0, 256)
+        quantize_h(apply_gain(closeness(512, 256), 256), 512, 256)
+        finish(256, 256)
+        quantize_h(apply_gain(closeness(768, SUB), SUB), 768, SUB)
+        quantize_h(apply_gain(closeness(896, SUB), SUB), 896, SUB)
+        finish(512, 256)
+        finish(768, SUB)
+        finish(896, SUB)

@@ -193,18 +193,21 @@ def tile_list_template_contact_gate_kernel(
         def x_operand(a, cols):
             return xq[a][:, cols].bitcast(FP8X4), xs[a][:, cols]
 
+        def d_weights(k, t):
+            if k == 2:
+                return w2w[:, 2 * t * P : 2 * (t + 1) * P].bitcast(FP4X4), w2s[:, t * P : (t + 1) * P]
+            return w1q[k][:, t * P : (t + 1) * P].bitcast(FP8X4), w1s[k][:, t * P : (t + 1) * P]
+
         def closeness(j0, width):
             absd = ring.tile([P, width * PACK], F32, name="absd")
             for s in range(width // SUB):
                 cols = slice(j0 + s * SUB, j0 + (s + 1) * SUB)
                 d = psum.tile([P, PACK, SUB], F32, name="d", bufs=4)
-                for a in range(2):
+                rhs = [x_operand(0, cols), x_operand(1, cols), (vw[cols.start].bitcast(FP8X4), vs[:, cols])]
+                order = (0, 1, 2) if j0 == 0 else (0, 2, 1)
+                for n, k in enumerate(order):
                     for t in range(PACK):
-                        w = slice(t * P, (t + 1) * P)
-                        mm(d[:, t, :], (w1q[a][:, w].bitcast(FP8X4), w1s[a][:, w]), x_operand(a, cols), a == 0 and t == 0, False)
-                for t in range(PACK):
-                    lhs = w2w[:, 2 * t * P : 2 * (t + 1) * P].bitcast(FP4X4), w2s[:, t * P : (t + 1) * P]
-                    mm(d[:, t, :], lhs, (vw[cols.start].bitcast(FP8X4), vs[:, cols]), False, t == PACK - 1)
+                        mm(d[:, t, :], d_weights(k, t), rhs[k], n == 0 and t == 0, n == 2 and t == PACK - 1)
                 nc.scalar.activation(
                     out=absd[:, s * SUB * PACK : (s + 1) * SUB * PACK].rearrange("p (j t) -> p j t", t=PACK),
                     in_=d[:].rearrange("p t j -> p j t"),
@@ -270,11 +273,8 @@ def tile_list_template_contact_gate_kernel(
         interleave_dealt(on_scalar, w1b[0][:], w1_raw[0][:])
         gather_x(4, 0, S)
         gather_x(5, 0, S)
-        cuts = [(0, CHUNK), (CHUNK, CHUNK), (HALF, HALF)]
-        xb1_all = held([P, PACK * S], BF16, "xb1", "w1_raw0")
-        xb1 = [xb1_all[:, PACK * j : PACK * (j + width)] for j, width in cuts]
-        for rounded, (j, width) in zip(xb1, cuts):
-            round_pair(on_scalar, rounded, 1, 0, j, width)
+        xb1_last = held([P, PACK * HALF], BF16, "xb1_last", "w1_raw0")
+        round_pair(on_scalar, xb1_last, 1, 0, HALF, HALF)
         interleave_dealt(on_scalar, w1b[1][:], w1_raw[1][:])
         behind5 = held([P, H + S], U8, "behind5", "plane5")
         w2s = behind5[:, :H]
@@ -285,17 +285,19 @@ def tile_list_template_contact_gate_kernel(
         gather_x(6, 0, S)
         w1s = [held([P, H], U8, "w1s0", "plane6")]
         quantize(w1q[0][:], w1s[0][:], w1b[0][:])
-        for rounded, (j, width) in zip(xb1, cuts):
-            gather_x(7, j, width)
-            round_pair(on_scalar, rounded, 1, 1, j, width)
+        gather_x(7, 0, CHUNK)
+        gather_x(7, CHUNK, CHUNK)
+        gather_x(7, HALF, HALF)
+        xb1 = [round_x(on_scalar, 1, j, CHUNK) for j in (0, CHUNK)]
+        round_pair(on_scalar, xb1_last, 1, 1, HALF, HALF)
         w1s.append(held([P, H], U8, "w1s1", "plane7"))
         quantize(w1q[1][:], w1s[1][:], w1b[1][:])
         quantize_x(1, 0, CHUNK, xb1[0])
         gather_words(0, CHUNK)
         quantize_x(1, CHUNK, CHUNK, xb1[1])
         gather_words(CHUNK, CHUNK, "w1b1")
-        gather_words(HALF, HALF)
-        quantize_x(1, HALF, HALF, xb1[2])
+        gather_words(HALF, HALF, "xb1_256")
+        quantize_x(1, HALF, HALF, xb1_last)
         round_w3(0, 256)
         round_w3(256, N)
         quantize_w3(0, 512)

@@ -181,10 +181,10 @@ def tile_list_template_contact_gate_kernel(
         def quantize_x(a, j, width, rounded):
             quantize(xq[a][:, j : j + width], xs[a][:, j : j + width], rounded[:])
 
-        def round_w3(c0, c1):
+        def round_w3_rest():
             on_vector(
-                out=w3b[:, 2 * PACK * c0 : 2 * PACK * c1].rearrange("p (a c e i) -> p a c i e", a=2, e=4, i=PACK),
-                in_=w3_raw[:, :, :, c0:c1].rearrange("p a i (c e) -> p a c i e", e=4),
+                out=w3b[:, PACK * 512 :].rearrange("p (a c e i) -> p a c i e", a=2, e=4, i=PACK),
+                in_=w3_raw[:, :, :, 256:].rearrange("p a i (c e) -> p a c i e", e=4),
             )
 
         def quantize_w3(j, width):
@@ -233,40 +233,38 @@ def tile_list_template_contact_gate_kernel(
         def quantize_h(hb, j, width):
             quantize(hq[:, j : j + width], hs[:, j : j + width], hb[:])
 
-        def project(copy, j):
-            cols = slice(j, j + SUB)
-            if j < HALF:
-                r = psum.tile([P, N_TILES, SUB], F32, name="r", bufs=2)
-            else:
-                r = psum.tile([P, N_TILES, SUB], F32, name="r", tag="d", bufs=4)
-            for m in range(N_TILES):
-                for a in range(2):
-                    first = 256 * a + P * m if m < 2 else 512 + P * a
-                    w = slice(first, first + P)
-                    mm(r[:, m, :], (w3q[:, w].bitcast(FP8X4), w3s[:, w]), x_operand(a, cols), a == 0, a == 1)
-            r_sb = r_all[j // HALF][:, j % HALF // SUB]
-            copy(out=r_sb, in_=r[:])
-            return r_sb
-
-        def finish(j0, width, copy=on_scalar):
-            projected = [project(copy, j) for j in range(j0, j0 + width, SUB)]
-            ob = ring.tile([P, N_TILES, width], F32, name="ob", bufs=3)
-            for s in range(width // SUB):
-                cols = slice(j0 + s * SUB, j0 + (s + 1) * SUB)
-                y = psum.tile([P, N_TILES, SUB], F32, name="y", bufs=2)
-                for m in range(N_TILES):
+        def finish(j0, r_tag, y_tag):
+            cols = slice(j0, j0 + CHUNK)
+            parts = [range(0, 2), range(2, N_TILES)]
+            projected = []
+            for part in parts:
+                r = psum.tile([P, len(part), CHUNK], F32, name="r", tag=r_tag, bufs=banks[r_tag])
+                for m in part:
+                    for a in range(2):
+                        first = 256 * a + P * m if m < 2 else 512 + P * a
+                        w = slice(first, first + P)
+                        mm(r[:, m - part.start, :], (w3q[:, w].bitcast(FP8X4), w3s[:, w]), x_operand(a, cols), a == 0, a == 1)
+                r_sb = held([P, len(part), CHUNK], F32, f"r_sb{j0}_{part.start}")
+                copy = on_vector if j0 == 0 else on_scalar
+                copy(out=r_sb[:], in_=r[:])
+                projected.append(r_sb)
+            for part, r_sb in zip(parts, projected):
+                y = psum.tile([P, len(part), CHUNK], F32, name="y", tag=y_tag, bufs=banks[y_tag])
+                for m in part:
                     w = slice(m * P, (m + 1) * P)
-                    mm(y[:, m, :], (w4w[:, w].bitcast(FP8X4), w4s[:, w]), (hq[:, cols].bitcast(FP8X4), hs[:, cols]), True, True)
-                nc.vector.tensor_tensor(ob[:, :, s * SUB : (s + 1) * SUB], y[:], projected[s], MULT)
-            nc.sync.dma_start(out=out_rows[:, :, j0 : j0 + width], in_=ob[:])
+                    rhs = hq[:, cols].bitcast(FP8X4), hs[:, cols]
+                    mm(y[:, m - part.start, :], (w4w[:, w].bitcast(FP8X4), w4s[:, w]), rhs, True, True)
+                ob = held([P, len(part), CHUNK], F32, f"ob{j0}_{part.start}")
+                nc.vector.tensor_tensor(ob[:], y[:], r_sb[:], MULT)
+                nc.sync.dma_start(out=out_rows[:, part.start : part.stop, cols], in_=ob[:])
 
+        banks = {"d": 4, "r": 2, "y": 2}
         for h in range(2):
             gather_x(0, HALF * h, HALF)
         for u in range(1, PACK):
             gather_x(u, 0, S)
-        r_all = [held([P, HALF // SUB, N_TILES, SUB], F32, f"r_all{h}", f"plane{h}") for h in range(2)]
         w3b = held([P, 2 * PACK * N], BF16, "w3b", "plane2")
-        xb0 = [held([P, PACK * HALF], BF16, f"xb0_{h}") for h in range(2)]
+        xb0 = [held([P, PACK * HALF], BF16, f"xb0_{h}", f"plane{h}") for h in range(2)]
         for u in range(2):
             for h in range(2):
                 round_pair(on_scalar, xb0[h], 0, u, HALF * h, HALF)
@@ -298,18 +296,18 @@ def tile_list_template_contact_gate_kernel(
         gather_words(CHUNK, CHUNK, "w1b1")
         gather_words(HALF, HALF, "xb1_256")
         quantize_x(1, HALF, HALF, xb1_last)
-        round_w3(0, 256)
-        round_w3(256, N)
+        for a, copy in enumerate((on_scalar, on_vector)):
+            interleave(copy, w3b[:, PACK * 256 * a : PACK * 256 * (a + 1)], w3_raw[:, a, :, :256])
+        round_w3_rest()
         quantize_w3(0, 512)
         hb = apply_gain(closeness(0, 256), 256, "w3_raw")
         quantize_w3(512, 256)
         quantize_h(hb, 0, 256)
         quantize_h(apply_gain(closeness(256, 256), 256), 256, 256)
-        finish(0, 256)
+        finish(0, "r", "y")
         quantize_h(apply_gain(closeness(512, 256), 256), 512, 256)
-        finish(256, 256)
         quantize_h(apply_gain(closeness(768, SUB), SUB), 768, SUB)
         quantize_h(apply_gain(closeness(896, SUB), SUB), 896, SUB)
-        finish(512, 256)
-        finish(768, SUB)
-        finish(896, SUB)
+        finish(256, "d", "y")
+        finish(512, "d", "d")
+        finish(768, "r", "y")

@@ -111,15 +111,10 @@ def tile_list_template_contact_gate_kernel(
         load_scale_rows(w2s_raw, w2_scales[0], 2)
         load_scale_rows(w2s_raw, w2_scales[0], 3)
         load_plane(3)
-        nc.sync.dma_start(out=gain_sb[:], in_=gain.rearrange("(p t) -> p t", t=PACK))
         load_plane(4)
-        load_scale_rows(w4s, w4_scales[0], 0)
         load_plane(5)
-        load_scale_rows(w4s, w4_scales[0], 1)
         nc.sync.dma_start(out=w1_raw[0][:], in_=w1_rows[0])
-        load_scale_rows(w4s, w4_scales[0], 2)
         load_plane(6)
-        load_scale_rows(w4s, w4_scales[0], 3)
         nc.sync.dma_start(out=w1_raw[1][:], in_=w1_rows[1])
         load_plane(7)
         load_words(tabw[:], tab_words[0].rearrange("p t i -> p (t i)"))
@@ -129,7 +124,10 @@ def tile_list_template_contact_gate_kernel(
         load_scale_rows(vs, vs_rows, 2)
         load_scale_rows(vs, vs_rows, 3)
         nc.sync.dma_start(out=w3_raw[:, 1], in_=w3_rows[1])
+        nc.sync.dma_start(out=gain_sb[:], in_=gain.rearrange("(p t) -> p t", t=PACK))
         load_words(w4w[:], w4_words[0].rearrange("p n i -> p (n i)"))
+        for q in range(4):
+            load_scale_rows(w4s, w4_scales[0], q)
 
         turned = psum.tile([P, P], F32, name="turned", tag="y", bufs=2)
         nc.tensor.transpose(turned[:], wgt_rows[:], ident[:])

@@ -212,7 +212,9 @@ def tile_list_template_contact_gate_kernel(
                     func=ACT.Abs,
                 )
             e = ring.tile([P, width * PACK], F32, name="e", bufs=3)
-            nc.scalar.activation(out=e[:], in_=absd[:], func=ACT.Exp, scale=-1.0)
+            step = PACK * (SUB if j0 == 0 else width)
+            for c in range(0, PACK * width, step):
+                nc.scalar.activation(out=e[:, c : c + step], in_=absd[:, c : c + step], func=ACT.Exp, scale=-1.0)
             return e
 
         def apply_gain(e, width, tag=None):
@@ -269,8 +271,10 @@ def tile_list_template_contact_gate_kernel(
         interleave_dealt(on_scalar, w1b[0][:], w1_raw[0][:])
         gather_x(4, 0, S)
         gather_x(5, 0, S)
-        xb1_last = held([P, PACK * HALF], BF16, "xb1_last", "w1_raw0")
+        xb1_paired = held([P, PACK * (HALF + CHUNK)], BF16, "xb1_paired", "w1_raw0")
+        xb1_last, xb1_first = xb1_paired[:, : PACK * HALF], xb1_paired[:, PACK * HALF :]
         round_pair(on_scalar, xb1_last, 1, 0, HALF, HALF)
+        round_pair(on_scalar, xb1_first, 1, 0, 0, CHUNK)
         interleave_dealt(on_scalar, w1b[1][:], w1_raw[1][:])
         behind5 = held([P, H + S], U8, "behind5", "plane5")
         w2s = behind5[:, :H]
@@ -284,7 +288,8 @@ def tile_list_template_contact_gate_kernel(
         gather_x(7, 0, CHUNK)
         gather_x(7, CHUNK, CHUNK)
         gather_x(7, HALF, HALF)
-        xb1 = [round_x(on_scalar, 1, j, CHUNK) for j in (0, CHUNK)]
+        round_pair(on_scalar, xb1_first, 1, 1, 0, CHUNK)
+        xb1 = [xb1_first, round_x(on_scalar, 1, CHUNK, CHUNK)]
         round_pair(on_scalar, xb1_last, 1, 1, HALF, HALF)
         w1s.append(held([P, H], U8, "w1s1", "plane7"))
         quantize(w1q[1][:], w1s[1][:], w1b[1][:])

@@ -112,8 +112,8 @@ def tile_list_template_contact_gate_kernel(
         load_scale_rows(w2s_raw, w2_scales[0], 3)
         load_plane(3)
         load_plane(4)
-        load_plane(5)
         nc.sync.dma_start(out=w1_raw[0][:], in_=w1_rows[0])
+        load_plane(5)
         load_plane(6)
         nc.sync.dma_start(out=w1_raw[1][:], in_=w1_rows[1])
         load_plane(7)
@@ -261,8 +261,10 @@ def tile_list_template_contact_gate_kernel(
         banks = {"d": 4, "r": 2, "y": 2}
         for h in range(2):
             gather_x(0, HALF * h, HALF)
-        for u in range(1, PACK):
+        for u in range(1, PACK - 1):
             gather_x(u, 0, S)
+        for h in range(2):
+            gather_x(PACK - 1, HALF * h, HALF)
         w3b = held([P, 2 * PACK * N], BF16, "w3b", "plane2")
         xb0 = [held([P, PACK * HALF], BF16, f"xb0_{h}", f"plane{h}") for h in range(2)]
         for u in range(2):
@@ -270,21 +272,22 @@ def tile_list_template_contact_gate_kernel(
                 round_pair(on_scalar, xb0[h], 0, u, HALF * h, HALF)
         interleave_dealt(on_scalar, w1b[0][:], w1_raw[0][:])
         gather_x(4, 0, S)
-        gather_x(5, 0, S)
+        behind4 = held([P, H + S], U8, "behind4", "plane4")
+        w2s = behind4[:, :H]
+        xs = (behind4[:, H:], xs1)
+        deal(w2s, w2s_raw[:])
+        for h in range(2):
+            quantize_x(0, HALF * h, HALF, xb0[h])
+        gather_x(5, HALF, HALF)
+        gather_x(5, 0, HALF)
         xb1_paired = held([P, PACK * (HALF + CHUNK)], BF16, "xb1_paired", "w1_raw0")
         xb1_last, xb1_first = xb1_paired[:, : PACK * HALF], xb1_paired[:, PACK * HALF :]
         round_pair(on_scalar, xb1_last, 1, 0, HALF, HALF)
         round_pair(on_scalar, xb1_first, 1, 0, 0, CHUNK)
         interleave_dealt(on_scalar, w1b[1][:], w1_raw[1][:])
-        behind5 = held([P, H + S], U8, "behind5", "plane5")
-        w2s = behind5[:, :H]
-        xs = (behind5[:, H:], xs1)
-        deal(w2s, w2s_raw[:])
-        for h in range(2):
-            quantize_x(0, HALF * h, HALF, xb0[h])
-        gather_x(6, 0, S)
-        w1s = [held([P, H], U8, "w1s0", "plane6")]
+        w1s = [held([P, H], U8, "w1s0", "plane5")]
         quantize(w1q[0][:], w1s[0][:], w1b[0][:])
+        gather_x(6, 0, S)
         gather_x(7, 0, CHUNK)
         gather_x(7, CHUNK, CHUNK)
         gather_x(7, HALF, HALF)

@@ -176,8 +176,13 @@ def tile_list_template_contact_gate_kernel(
                 in_=picked[a][:, 2 * u : 2 * u + 2, j : j + width].rearrange("p i c -> p c i"),
             )
 
+        def x_scales(a, j, width):
+            if a == 1:
+                return xs1[:, j : j + width]
+            return xs0[j // HALF][:, j % HALF : j % HALF + width]
+
         def quantize_x(a, j, width, rounded):
-            quantize(xq[a][:, j : j + width], xs[a][:, j : j + width], rounded[:])
+            quantize(xq[a][:, j : j + width], x_scales(a, j, width), rounded[:])
 
         def round_w3_rest():
             on_vector(
@@ -189,7 +194,7 @@ def tile_list_template_contact_gate_kernel(
             quantize(w3q[:, j : j + width], w3s[:, j : j + width], w3b[:, PACK * j : PACK * (j + width)])
 
         def x_operand(a, cols):
-            return xq[a][:, cols].bitcast(FP8X4), xs[a][:, cols]
+            return xq[a][:, cols].bitcast(FP8X4), x_scales(a, cols.start, cols.stop - cols.start)
 
         def d_weights(k, t):
             if k == 2:
@@ -245,7 +250,7 @@ def tile_list_template_contact_gate_kernel(
                         w = slice(first, first + P)
                         mm(r[:, m - part.start, :], (w3q[:, w].bitcast(FP8X4), w3s[:, w]), x_operand(a, cols), a == 0, a == 1)
                 r_sb = held([P, len(part), CHUNK], F32, f"r_sb{j0}_{part.start}")
-                copy = on_vector if j0 == 0 else on_scalar
+                copy = on_vector if j0 == 0 and part.start == 0 else on_scalar
                 copy(out=r_sb[:], in_=r[:])
                 projected.append(r_sb)
             for part, r_sb in zip(parts, projected):
@@ -272,12 +277,11 @@ def tile_list_template_contact_gate_kernel(
                 round_pair(on_scalar, xb0[h], 0, u, HALF * h, HALF)
         interleave_dealt(on_scalar, w1b[0][:], w1_raw[0][:])
         gather_x(4, 0, S)
-        behind4 = held([P, H + S], U8, "behind4", "plane4")
+        behind4 = held([P, H + HALF], U8, "behind4", "plane4")
         w2s = behind4[:, :H]
-        xs = (behind4[:, H:], xs1)
         deal(w2s, w2s_raw[:])
-        for h in range(2):
-            quantize_x(0, HALF * h, HALF, xb0[h])
+        xs0 = [behind4[:, H:]]
+        quantize_x(0, 0, HALF, xb0[0])
         gather_x(5, HALF, HALF)
         gather_x(5, 0, HALF)
         xb1_paired = held([P, PACK * (HALF + CHUNK)], BF16, "xb1_paired", "w1_raw0")
@@ -285,9 +289,12 @@ def tile_list_template_contact_gate_kernel(
         round_pair(on_scalar, xb1_last, 1, 0, HALF, HALF)
         round_pair(on_scalar, xb1_first, 1, 0, 0, CHUNK)
         interleave_dealt(on_scalar, w1b[1][:], w1_raw[1][:])
-        w1s = [held([P, H], U8, "w1s0", "plane5")]
-        quantize(w1q[0][:], w1s[0][:], w1b[0][:])
         gather_x(6, 0, S)
+        behind6 = held([P, H + HALF], U8, "behind6", "plane6")
+        xs0.append(behind6[:, H:])
+        w1s = [behind6[:, :H]]
+        quantize_x(0, HALF, HALF, xb0[1])
+        quantize(w1q[0][:], w1s[0][:], w1b[0][:])
         gather_x(7, 0, CHUNK)
         gather_x(7, CHUNK, CHUNK)
         gather_x(7, HALF, HALF)

@@ -31,12 +31,15 @@ def tile_list_template_contact_gate_kernel(
     nc = tc.nc
     with ExitStack() as ctx:
         keep = ctx.enter_context(tc.tile_pool(name="keep", bufs=1))
-        ring = ctx.enter_context(tc.tile_pool(name="ring", bufs=2))
+        turns = ctx.enter_context(tc.tile_pool(name="turns", bufs=1))
         psum = ctx.enter_context(tc.psum_pool(name="psum", bufs=1))
         on_vector, on_scalar = nc.vector.tensor_copy, nc.scalar.copy
 
         def held(shape, dtype, name, tag=None):
             return keep.tile(shape, dtype, name=name, tag=tag or name, align_bytes=64)
+
+        def placed(shape, dtype, name, offset):
+            return turns.tile(shape, dtype, name=name, offset=offset, align_bytes=64)
 
         def load_words(tile, rows):
             nc.sync.dma_start(out=tile.bitcast(I32), in_=rows.bitcast(I32))
@@ -72,14 +75,14 @@ def tile_list_template_contact_gate_kernel(
         wgt_rows = held([P, P], F32, "wgt_rows")
         wgt_sb = held([P, S], F32, "wgt_sb")
         planes = [held([P, T], F32, f"plane{u}") for u in range(8)]
-        w1_raw = [held([P, PACK, H], F32, f"w1_raw{a}") for a in range(2)]
+        w1_raw = [placed([P, PACK, H], F32, "w1_raw0", 6144), held([P, PACK, H], F32, "w1_raw1")]
         w3_raw = held([P, 2, PACK, N], F32, "w3_raw")
         w2w_raw = held([P, 2 * H], U8, "w2w_raw")
         w2s_raw = held([P, H], U8, "w2s_raw")
         w2w = held([P, 2 * H], U8, "w2w")
         w4w = held([P, N], U32, "w4w")
         w4s = held([P, N], U8, "w4s")
-        gain_sb = held([P, PACK], F32, "gain_sb")
+        gain_row = held([P, PACK * CHUNK], F32, "gain_row")
         ident = held([P, P], F32, "ident")
         vs_rows = held([P, S], U8, "vs_rows")
         vs = held([P, S], U8, "vs")
@@ -104,7 +107,22 @@ def tile_list_template_contact_gate_kernel(
         deal(w2w[:].bitcast(U16), w2w_raw[:].bitcast(U16))
         on_vector(vs_rows[:], tabs[:].indirect(offs_sb[:]))
         nc.sync.dma_start(offs2_sb[:], offs2)
+
+        turned = psum.tile([P, P], F32, name="turned", tag="bank6")
+        nc.tensor.transpose(turned[:], wgt_rows[:], ident[:])
+        for h in range(2):
+            spread = held([P, 4, P], F32, f"spread{h}")
+            on_scalar(
+                out=spread[:].rearrange("j b (q e) -> j b q e", e=8),
+                in_=turned[:].rearrange("j (q b) -> j b q", b=8)[:, 4 * h : 4 * h + 4, :].unsqueeze(3).to_broadcast([P, 4, 16, 8]),
+            )
+            back = psum.tile([P, 4, P], F32, name="back", tag=f"bank{4 + h}")
+            for b in range(4):
+                nc.tensor.transpose(back[:, b, :], spread[:, b, :], ident[:])
+            on_scalar(out=wgt_sb[:, HALF * h : HALF * (h + 1)], in_=back[:].rearrange("p b j -> p (b j)"))
+
         load_plane(1)
+        nc.sync.dma_start(out=wgt_rows[:, :PACK], in_=gain.rearrange("(p t) -> p t", t=PACK))
         load_scale_rows(w2s_raw, w2_scales[0], 0)
         load_scale_rows(w2s_raw, w2_scales[0], 1)
         load_plane(2)
@@ -124,23 +142,20 @@ def tile_list_template_contact_gate_kernel(
         load_scale_rows(vs, vs_rows, 2)
         load_scale_rows(vs, vs_rows, 3)
         nc.sync.dma_start(out=w3_raw[:, 1], in_=w3_rows[1])
-        nc.sync.dma_start(out=gain_sb[:], in_=gain.rearrange("(p t) -> p t", t=PACK))
         load_words(w4w[:], w4_words[0].rearrange("p n i -> p (n i)"))
         for q in range(4):
             load_scale_rows(w4s, w4_scales[0], q)
 
-        turned = psum.tile([P, P], F32, name="turned", tag="y", bufs=2)
-        nc.tensor.transpose(turned[:], wgt_rows[:], ident[:])
-        for h in range(2):
-            spread = held([P, 4, P], F32, f"spread{h}")
-            on_scalar(
-                out=spread[:].rearrange("j b (q e) -> j b q e", e=8),
-                in_=turned[:].rearrange("j (q b) -> j b q", b=8)[:, 4 * h : 4 * h + 4, :].unsqueeze(3).to_broadcast([P, 4, 16, 8]),
-            )
-            back = psum.tile([P, 4, P], F32, name="back", tag="r", bufs=2)
-            for b in range(4):
-                nc.tensor.transpose(back[:, b, :], spread[:, b, :], ident[:])
-            on_scalar(out=wgt_sb[:, HALF * h : HALF * (h + 1)], in_=back[:].rearrange("p b j -> p (b j)"))
+        gain_turned = psum.tile([P, P], F32, name="gain_turned", tag="bank3")
+        nc.tensor.transpose(gain_turned[:], wgt_rows[:], ident[:])
+        gain_rows = held([P, P], F32, "gain_rows", "spread0")
+        on_scalar(out=gain_rows[:], in_=gain_turned[:])
+        gain_bank = psum.tile([P, P], F32, name="gain_bank")
+        nc.tensor.transpose(gain_bank[:], gain_rows[:], ident[:])
+        on_scalar(
+            out=gain_row[:].rearrange("p (j t) -> p j t", t=PACK),
+            in_=wgt_rows[:, :PACK].unsqueeze(1).to_broadcast([P, CHUNK, PACK]),
+        )
 
         picked = [held([P, PACK, S], F32, f"picked{a}") for a in range(2)]
         xq = [held([P, S], U32, f"xq{a}") for a in range(2)]
@@ -148,9 +163,9 @@ def tile_list_template_contact_gate_kernel(
         w1b = [held([P, PACK * H], BF16, f"w1b{a}") for a in range(2)]
         w3q = held([P, 2 * N], U32, "w3q")
         w3s = held([P, 2 * N], U8, "w3s")
-        xs1 = held([P, S], U8, "xs1")
+        xs1 = held([P, 768], U8, "xs1")
+        xs1_last = []
         hq = held([P, S], U32, "hq")
-        hs = held([P, S], U8, "hs")
         vw = {}
         out_rows = out.rearrange("(m p) j -> p m j", p=P)
 
@@ -159,8 +174,8 @@ def tile_list_template_contact_gate_kernel(
             dst = picked[u // PACK][:, u % PACK, j : j + width]
             nc.vector.tensor_tensor(dst, planes[u][:].indirect(lists), wgt_sb[:, j : j + width], MULT)
 
-        def gather_words(j, width, tag=None):
-            words = held([P, width], U32, f"vw{j}", tag)
+        def gather_words(j, words):
+            width = words.shape[1]
             on_vector(words[:], tabw[:].indirect(offs_sb[:, j // 16 : (j + width) // 16]))
             for s in range(0, width, SUB):
                 vw[j + s] = words[:, s : s + SUB]
@@ -178,7 +193,7 @@ def tile_list_template_contact_gate_kernel(
 
         def x_scales(a, j, width):
             if a == 1:
-                return xs1[:, j : j + width]
+                return xs1[:, j : j + width] if j < 768 else xs1_last[0][:, j - 768 : j - 768 + width]
             return xs0[j // HALF][:, j % HALF : j % HALF + width]
 
         def quantize_x(a, j, width, rounded):
@@ -186,12 +201,12 @@ def tile_list_template_contact_gate_kernel(
 
         def round_w3_rest():
             on_vector(
-                out=w3b[:, PACK * 512 :].rearrange("p (a c e i) -> p a c i e", a=2, e=4, i=PACK),
+                out=w3b_rest[:].rearrange("p (a c e i) -> p a c i e", a=2, e=4, i=PACK),
                 in_=w3_raw[:, :, :, 256:].rearrange("p a i (c e) -> p a c i e", e=4),
             )
 
-        def quantize_w3(j, width):
-            quantize(w3q[:, j : j + width], w3s[:, j : j + width], w3b[:, PACK * j : PACK * (j + width)])
+        def quantize_w3(j, width, rounded):
+            quantize(w3q[:, j : j + width], w3s[:, j : j + width], rounded[:])
 
         def x_operand(a, cols):
             return xq[a][:, cols].bitcast(FP8X4), x_scales(a, cols.start, cols.stop - cols.start)
@@ -201,76 +216,65 @@ def tile_list_template_contact_gate_kernel(
                 return w2w[:, 2 * t * P : 2 * (t + 1) * P].bitcast(FP4X4), w2s[:, t * P : (t + 1) * P]
             return w1q[k][:, t * P : (t + 1) * P].bitcast(FP8X4), w1s[k][:, t * P : (t + 1) * P]
 
-        def closeness(j0, width):
-            absd = ring.tile([P, width * PACK], F32, name="absd")
-            for s in range(width // SUB):
-                cols = slice(j0 + s * SUB, j0 + (s + 1) * SUB)
-                d = psum.tile([P, PACK, SUB], F32, name="d", bufs=4)
-                rhs = [x_operand(0, cols), x_operand(1, cols), (vw[cols.start].bitcast(FP8X4), vs[:, cols])]
-                order = (0, 1, 2) if j0 == 0 else (0, 2, 1)
-                for n, k in enumerate(order):
-                    for t in range(PACK):
-                        mm(d[:, t, :], d_weights(k, t), rhs[k], n == 0 and t == 0, n == 2 and t == PACK - 1)
-                nc.scalar.activation(
-                    out=absd[:, s * SUB * PACK : (s + 1) * SUB * PACK].rearrange("p (j t) -> p j t", t=PACK),
-                    in_=d[:].rearrange("p t j -> p j t"),
-                    func=ACT.Abs,
-                )
-            e = ring.tile([P, width * PACK], F32, name="e", bufs=3)
-            step = PACK * (SUB if j0 == 0 else width)
-            for c in range(0, PACK * width, step):
-                nc.scalar.activation(out=e[:, c : c + step], in_=absd[:, c : c + step], func=ACT.Exp, scale=-1.0)
-            return e
+        def distance(j, bank, absd):
+            cols = slice(j, j + SUB)
+            d = psum.tile([P, PACK, SUB], F32, name="d", tag=f"bank{bank}")
+            rhs = [x_operand(0, cols), x_operand(1, cols), (vw[j].bitcast(FP8X4), vs[:, cols])]
+            order = (0, 1, 2) if j < CHUNK else (0, 2, 1)
+            for n, k in enumerate(order):
+                for t in range(PACK):
+                    mm(d[:, t, :], d_weights(k, t), rhs[k], n == 0 and t == 0, n == 2 and t == PACK - 1)
+            nc.scalar.activation(out=absd.rearrange("p (j t) -> p j t", t=PACK), in_=d[:].rearrange("p t j -> p j t"), func=ACT.Abs)
 
-        def apply_gain(e, width, tag=None):
-            if tag:
-                hb = held([P, width * PACK], BF16, "hb_first", tag)
-            else:
-                hb = ring.tile([P, width * PACK], BF16, name="hb", align_bytes=64)
+        def decay(e, absd):
+            nc.scalar.activation(out=e, in_=absd, func=ACT.Exp, scale=-1.0)
+
+        def gain_on_vector(dst, e):
             nc.vector.tensor_tensor(
-                hb[:].rearrange("p (j t) -> p j t", t=PACK),
-                e[:].rearrange("p (j t) -> p j t", t=PACK),
-                gain_sb[:].unsqueeze(1).to_broadcast([P, width, PACK]),
+                dst.rearrange("p (j t) -> p j t", t=PACK),
+                e.rearrange("p (j t) -> p j t", t=PACK),
+                gain_bank[:, :PACK].unsqueeze(1).to_broadcast([P, e.shape[1] // PACK, PACK]),
                 MULT,
             )
-            return hb
 
-        def quantize_h(hb, j, width):
-            quantize(hq[:, j : j + width], hs[:, j : j + width], hb[:])
+        def gain_on_gpsimd(dst, e):
+            nc.gpsimd.tensor_tensor(dst, e, gain_row[:, : e.shape[1]], MULT)
 
-        def finish(j0, r_tag, y_tag):
+        def quantize_h(j, width, scales, rounded):
+            quantize(hq[:, j : j + width], scales, rounded)
+
+        parts = [range(0, 2), range(2, N_TILES)]
+
+        def project(bank, copy, r_sb, pieces):
+            r = psum.tile([P, len(pieces), CHUNK], F32, name="r", tag=f"bank{bank}")
+            for n, (j0, m) in enumerate(pieces):
+                for a in range(2):
+                    first = 256 * a + P * m if m < 2 else 512 + P * a
+                    w = slice(first, first + P)
+                    mm(r[:, n, :], (w3q[:, w].bitcast(FP8X4), w3s[:, w]), x_operand(a, slice(j0, j0 + CHUNK)), a == 0, a == 1)
+            copy(out=r_sb, in_=r[:])
+
+        def finish(j0, banks, projected, scales, staged=None):
+            staged = staged if staged is not None else held([P, N_TILES, CHUNK], F32, f"ob{j0}")
             cols = slice(j0, j0 + CHUNK)
-            parts = [range(0, 2), range(2, N_TILES)]
-            projected = []
-            for part in parts:
-                r = psum.tile([P, len(part), CHUNK], F32, name="r", tag=r_tag, bufs=banks[r_tag])
-                for m in part:
-                    for a in range(2):
-                        first = 256 * a + P * m if m < 2 else 512 + P * a
-                        w = slice(first, first + P)
-                        mm(r[:, m - part.start, :], (w3q[:, w].bitcast(FP8X4), w3s[:, w]), x_operand(a, cols), a == 0, a == 1)
-                r_sb = held([P, len(part), CHUNK], F32, f"r_sb{j0}_{part.start}")
-                copy = on_vector if j0 == 0 and part.start == 0 else on_scalar
-                copy(out=r_sb[:], in_=r[:])
-                projected.append(r_sb)
-            for part, r_sb in zip(parts, projected):
-                y = psum.tile([P, len(part), CHUNK], F32, name="y", tag=y_tag, bufs=banks[y_tag])
+            for part, bank, r_sb in zip(parts, banks, projected):
+                y = psum.tile([P, len(part), CHUNK], F32, name="y", tag=f"bank{bank}")
                 for m in part:
                     w = slice(m * P, (m + 1) * P)
-                    rhs = hq[:, cols].bitcast(FP8X4), hs[:, cols]
+                    rhs = hq[:, cols].bitcast(FP8X4), scales
                     mm(y[:, m - part.start, :], (w4w[:, w].bitcast(FP8X4), w4s[:, w]), rhs, True, True)
-                ob = held([P, len(part), CHUNK], F32, f"ob{j0}_{part.start}")
-                nc.vector.tensor_tensor(ob[:], y[:], r_sb[:], MULT)
-                nc.sync.dma_start(out=out_rows[:, part.start : part.stop, cols], in_=ob[:])
+                ob = staged[:, part.start : part.stop]
+                nc.vector.tensor_tensor(ob, y[:], r_sb, MULT)
+                nc.sync.dma_start(out=out_rows[:, part.start : part.stop, cols], in_=ob)
 
-        banks = {"d": 4, "r": 2, "y": 2}
         for h in range(2):
             gather_x(0, HALF * h, HALF)
         for u in range(1, PACK - 1):
             gather_x(u, 0, S)
         for h in range(2):
             gather_x(PACK - 1, HALF * h, HALF)
-        w3b = held([P, 2 * PACK * N], BF16, "w3b", "plane2")
+        w3b = placed([P, PACK * 512], BF16, "w3b", 0)
+        w3b_rest = placed([P, PACK * 256], BF16, "w3b_rest", 4096)
         xb0 = [held([P, PACK * HALF], BF16, f"xb0_{h}", f"plane{h}") for h in range(2)]
         for u in range(2):
             for h in range(2):
@@ -284,7 +288,7 @@ def tile_list_template_contact_gate_kernel(
         quantize_x(0, 0, HALF, xb0[0])
         gather_x(5, HALF, HALF)
         gather_x(5, 0, HALF)
-        xb1_paired = held([P, PACK * (HALF + CHUNK)], BF16, "xb1_paired", "w1_raw0")
+        xb1_paired = placed([P, PACK * (HALF + CHUNK)], BF16, "xb1_paired", 6144)
         xb1_last, xb1_first = xb1_paired[:, : PACK * HALF], xb1_paired[:, PACK * HALF :]
         round_pair(on_scalar, xb1_last, 1, 0, HALF, HALF)
         round_pair(on_scalar, xb1_first, 1, 0, 0, CHUNK)
@@ -304,23 +308,59 @@ def tile_list_template_contact_gate_kernel(
         w1s.append(held([P, H], U8, "w1s1", "plane7"))
         quantize(w1q[1][:], w1s[1][:], w1b[1][:])
         quantize_x(1, 0, CHUNK, xb1[0])
-        gather_words(0, CHUNK)
+        gather_words(0, held([P, CHUNK], U32, "vw0"))
         quantize_x(1, CHUNK, CHUNK, xb1[1])
-        gather_words(CHUNK, CHUNK, "w1b1")
-        gather_words(HALF, HALF, "xb1_256")
-        quantize_x(1, HALF, HALF, xb1_last)
+        gather_words(CHUNK, held([P, CHUNK], U32, "vw256", "w1b1"))
+        gather_words(HALF, held([P, CHUNK], U32, "vw512", "xb1_256"))
+        quantize_x(1, HALF, CHUNK, xb1_last[:, : PACK * CHUNK])
         for a, copy in enumerate((on_scalar, on_vector)):
             interleave(copy, w3b[:, PACK * 256 * a : PACK * 256 * (a + 1)], w3_raw[:, a, :, :256])
         round_w3_rest()
-        quantize_w3(0, 512)
-        hb = apply_gain(closeness(0, 256), 256, "w3_raw")
-        quantize_w3(512, 256)
-        quantize_h(hb, 0, 256)
-        quantize_h(apply_gain(closeness(256, 256), 256), 256, 256)
-        finish(0, "r", "y")
-        quantize_h(apply_gain(closeness(512, 256), 256), 512, 256)
-        quantize_h(apply_gain(closeness(768, SUB), SUB), 768, SUB)
-        quantize_h(apply_gain(closeness(896, SUB), SUB), 896, SUB)
-        finish(256, "d", "y")
-        finish(512, "d", "d")
-        finish(768, "r", "y")
+        quantize_w3(0, 512, w3b)
+        quantize_w3(512, 256, w3b_rest)
+        gather_words(768, placed([P, CHUNK], U32, "vw768", 256))
+        xs1_last.append(placed([P, CHUNK], U8, "xs1_last", 0))
+        quantize_x(1, 768, CHUNK, xb1_last[:, PACK * CHUNK :])
+        absd = [held([P, CHUNK * PACK], F32, f"absd{c}", f"plane{c}") for c in range(4)]
+        e0, e1, e2, e3 = decayed = [held([P, CHUNK * PACK], F32, f"e{c}") for c in range(4)]
+        halves = [slice(0, PACK * SUB), slice(PACK * SUB, PACK * CHUNK)]
+        for c in range(4):
+            for s in range(2):
+                distance(CHUNK * c + SUB * s, (2 * c + s) % 7, absd[c][:, halves[s]])
+            for half in halves:
+                decay(decayed[c][:, half], absd[c][:, half])
+        hs = held([P, S], U8, "hs")
+        hb0 = placed([P, PACK * CHUNK], BF16, "hb0", 6144)
+        gain_on_vector(hb0[:, :576], e0[:, :576])
+        gain_on_gpsimd(hb0[:, 576:], e0[:, 576:])
+        r0 = held([P, 2, CHUNK], F32, "r0a")[:], held([P, 1, CHUNK], F32, "r0b")[:]
+        project(1, on_vector, r0[0], [(0, 0), (0, 1)])
+        project(2, on_vector, r0[1], [(0, 2)])
+        quantize_h(0, CHUNK, hs[:, :CHUNK], hb0[:])
+        hb1 = placed([P, PACK * CHUNK], BF16, "hb1", 6144)
+        gain_on_gpsimd(hb1[:, 320:], e1[:, 320:])
+        r_last = held([P, 7, CHUNK], F32, "r_last", "plane3")
+        r1 = placed([P, 2, CHUNK], F32, "r1a", 10240)[:], r_last[:, 6:]
+        project(3, on_vector, r1[0], [(256, 0), (256, 1)])
+        project(4, on_scalar, r1[1], [(256, 2)])
+        gain_on_vector(hb1[:, :320], e1[:, :320])
+        hb2 = placed([P, PACK * CHUNK], BF16, "hb2", 8192)
+        for half in halves:
+            gain_on_vector(hb2[:, half], e2[:, half])
+        hs1 = held([P, CHUNK], U8, "hs1", "e2")
+        quantize_h(256, CHUNK, hs1[:], hb1[:])
+        quantize_h(512, CHUNK, hs[:, 512:768], hb2[:])
+        hb3 = placed([P, PACK * SUB], BF16, "hb3", 7680)
+        gain_on_gpsimd(hb3[:], e3[:, : PACK * SUB])
+        finish(0, (1, 2), r0, hs[:, :CHUNK], placed([P, N_TILES, CHUNK], F32, "ob0", 3584))
+        finish(256, (5, 3), r1, hs1[:])
+        hb4 = placed([P, PACK * SUB], BF16, "hb4", 10240)
+        gain_on_vector(hb4[:], e3[:, PACK * SUB :])
+        quantize_h(768, SUB, hs[:, 768:896], hb3[:])
+        quantize_h(896, SUB, hs[:, 896:], hb4[:])
+        r2, r3 = (r_last[:, 0:2], r_last[:, 2:3]), (r_last[:, 4:6], r_last[:, 3:4])
+        project(6, on_scalar, r_last[:, 0:2], [(512, 0), (512, 1)])
+        project(0, on_scalar, r_last[:, 2:4], [(512, 2), (768, 2)])
+        project(1, on_scalar, r_last[:, 4:6], [(768, 0), (768, 1)])
+        finish(512, (4, 2), r2, hs[:, 512:768], placed([P, N_TILES, CHUNK], F32, "ob512", 7168))
+        finish(768, (5, 3), r3, hs[:, 768:])

@@ -70,7 +70,7 @@ def tile_list_template_contact_gate_kernel(
 
         offs_sb = held([P, S // 16], U16, "offs_sb")
         offs2_sb = held([P, S // 16], U16, "offs2_sb")
-        tabw = held([P, T], U32, "tabw")
+        tabw = placed([P, T], U32, "tabw", 14336)
         tabs = held([P, T], U8, "tabs")
         wgt_rows = held([P, P], F32, "wgt_rows")
         wgt_sb = held([P, S], F32, "wgt_sb")
@@ -110,8 +110,8 @@ def tile_list_template_contact_gate_kernel(
 
         turned = psum.tile([P, P], F32, name="turned", tag="bank6")
         nc.tensor.transpose(turned[:], wgt_rows[:], ident[:])
-        for h in range(2):
-            spread = held([P, 4, P], F32, f"spread{h}")
+        spreads = [held([P, 4, P], F32, f"spread{h}") for h in range(2)]
+        for h, spread in enumerate(spreads):
             on_scalar(
                 out=spread[:].rearrange("j b (q e) -> j b q e", e=8),
                 in_=turned[:].rearrange("j (q b) -> j b q", b=8)[:, 4 * h : 4 * h + 4, :].unsqueeze(3).to_broadcast([P, 4, 16, 8]),
@@ -122,7 +122,8 @@ def tile_list_template_contact_gate_kernel(
             on_scalar(out=wgt_sb[:, HALF * h : HALF * (h + 1)], in_=back[:].rearrange("p b j -> p (b j)"))
 
         load_plane(1)
-        nc.sync.dma_start(out=wgt_rows[:, :PACK], in_=gain.rearrange("(p t) -> p t", t=PACK))
+        gain_line = spreads[0][:].rearrange("j b p -> j (b p)")
+        nc.sync.dma_start(out=gain_line[:1, :], in_=gain.unsqueeze(0))
         load_scale_rows(w2s_raw, w2_scales[0], 0)
         load_scale_rows(w2s_raw, w2_scales[0], 1)
         load_plane(2)
@@ -146,15 +147,12 @@ def tile_list_template_contact_gate_kernel(
         for q in range(4):
             load_scale_rows(w4s, w4_scales[0], q)
 
-        gain_turned = psum.tile([P, P], F32, name="gain_turned", tag="bank3")
-        nc.tensor.transpose(gain_turned[:], wgt_rows[:], ident[:])
-        gain_rows = held([P, P], F32, "gain_rows", "spread0")
-        on_scalar(out=gain_rows[:], in_=gain_turned[:])
-        gain_bank = psum.tile([P, P], F32, name="gain_bank")
-        nc.tensor.transpose(gain_bank[:], gain_rows[:], ident[:])
+        gain_bank = psum.tile([P, P + PACK], F32, name="gain_bank")
+        for t in range(PACK):
+            nc.tensor.transpose(gain_bank[:, t : t + P], gain_line[:, t::PACK], ident[:])
         on_scalar(
             out=gain_row[:].rearrange("p (j t) -> p j t", t=PACK),
-            in_=wgt_rows[:, :PACK].unsqueeze(1).to_broadcast([P, CHUNK, PACK]),
+            in_=gain_bank[:, :PACK].unsqueeze(1).to_broadcast([P, CHUNK, PACK]),
         )
 
         picked = [held([P, PACK, S], F32, f"picked{a}") for a in range(2)]
@@ -220,7 +218,7 @@ def tile_list_template_contact_gate_kernel(
             cols = slice(j, j + SUB)
             d = psum.tile([P, PACK, SUB], F32, name="d", tag=f"bank{bank}")
             rhs = [x_operand(0, cols), x_operand(1, cols), (vw[j].bitcast(FP8X4), vs[:, cols])]
-            order = (0, 1, 2) if j < CHUNK else (0, 2, 1)
+            order = (0, 1, 2) if j < CHUNK or j == S - SUB else (0, 2, 1)
             for n, k in enumerate(order):
                 for t in range(PACK):
                     mm(d[:, t, :], d_weights(k, t), rhs[k], n == 0 and t == 0, n == 2 and t == PACK - 1)
@@ -254,18 +252,20 @@ def tile_list_template_contact_gate_kernel(
                     mm(r[:, n, :], (w3q[:, w].bitcast(FP8X4), w3s[:, w]), x_operand(a, slice(j0, j0 + CHUNK)), a == 0, a == 1)
             copy(out=r_sb, in_=r[:])
 
-        def finish(j0, banks, projected, scales, staged=None):
-            staged = staged if staged is not None else held([P, N_TILES, CHUNK], F32, f"ob{j0}")
-            cols = slice(j0, j0 + CHUNK)
-            for part, bank, r_sb in zip(parts, banks, projected):
-                y = psum.tile([P, len(part), CHUNK], F32, name="y", tag=f"bank{bank}")
-                for m in part:
-                    w = slice(m * P, (m + 1) * P)
-                    rhs = hq[:, cols].bitcast(FP8X4), scales
-                    mm(y[:, m - part.start, :], (w4w[:, w].bitcast(FP8X4), w4s[:, w]), rhs, True, True)
-                ob = staged[:, part.start : part.stop]
-                nc.vector.tensor_tensor(ob, y[:], r_sb, MULT)
-                nc.sync.dma_start(out=out_rows[:, part.start : part.stop, cols], in_=ob)
+        def finish(j0, part, bank, r_sb, scales, ob):
+            cols, rows = slice(j0, j0 + CHUNK), parts[part]
+            y = psum.tile([P, len(rows), CHUNK], F32, name="y", tag=f"bank{bank}")
+            for m in rows:
+                w = slice(m * P, (m + 1) * P)
+                rhs = hq[:, cols].bitcast(FP8X4), scales
+                mm(y[:, m - rows.start, :], (w4w[:, w].bitcast(FP8X4), w4s[:, w]), rhs, True, True)
+            nc.vector.tensor_tensor(ob, y[:], r_sb, MULT)
+            nc.sync.dma_start(out=out_rows[:, rows.start : rows.stop, cols], in_=ob)
+
+        def finish_both(j0, banks, projected, scales, tag=None):
+            staged = held([P, N_TILES, CHUNK], F32, f"ob{j0}", tag)
+            for part, rows in enumerate(parts):
+                finish(j0, part, banks[part], projected[part], scales, staged[:, rows.start : rows.stop])
 
         for h in range(2):
             gather_x(0, HALF * h, HALF)
@@ -288,7 +288,7 @@ def tile_list_template_contact_gate_kernel(
         quantize_x(0, 0, HALF, xb0[0])
         gather_x(5, HALF, HALF)
         gather_x(5, 0, HALF)
-        xb1_paired = placed([P, PACK * (HALF + CHUNK)], BF16, "xb1_paired", 6144)
+        xb1_paired = placed([P, PACK * (HALF + CHUNK)], BF16, "xb1_paired", 8192)
         xb1_last, xb1_first = xb1_paired[:, : PACK * HALF], xb1_paired[:, PACK * HALF :]
         round_pair(on_scalar, xb1_last, 1, 0, HALF, HALF)
         round_pair(on_scalar, xb1_first, 1, 0, 0, CHUNK)
@@ -318,49 +318,54 @@ def tile_list_template_contact_gate_kernel(
         round_w3_rest()
         quantize_w3(0, 512, w3b)
         quantize_w3(512, 256, w3b_rest)
-        gather_words(768, placed([P, CHUNK], U32, "vw768", 256))
+        gather_words(768, placed([P, SUB], U32, "vw768", 256))
         xs1_last.append(placed([P, CHUNK], U8, "xs1_last", 0))
         quantize_x(1, 768, CHUNK, xb1_last[:, PACK * CHUNK :])
         absd = [held([P, CHUNK * PACK], F32, f"absd{c}", f"plane{c}") for c in range(4)]
         e0, e1, e2, e3 = decayed = [held([P, CHUNK * PACK], F32, f"e{c}") for c in range(4)]
         halves = [slice(0, PACK * SUB), slice(PACK * SUB, PACK * CHUNK)]
-        for c in range(4):
+        for c in range(3):
             for s in range(2):
-                distance(CHUNK * c + SUB * s, (2 * c + s) % 7, absd[c][:, halves[s]])
+                distance(CHUNK * c + SUB * s, 2 * c + s, absd[c][:, halves[s]])
             for half in halves:
                 decay(decayed[c][:, half], absd[c][:, half])
+        distance(768, 6, absd[3][:, halves[0]])
         hs = held([P, S], U8, "hs")
-        hb0 = placed([P, PACK * CHUNK], BF16, "hb0", 6144)
-        gain_on_vector(hb0[:, :576], e0[:, :576])
-        gain_on_gpsimd(hb0[:, 576:], e0[:, 576:])
-        r0 = held([P, 2, CHUNK], F32, "r0a")[:], held([P, 1, CHUNK], F32, "r0b")[:]
+        hb0 = placed([P, PACK * CHUNK], BF16, "hb0", 12288)
+        gain_on_vector(hb0[:, :512], e0[:, :512])
+        gain_on_gpsimd(hb0[:, 512:], e0[:, 512:])
+        r0 = held([P, 2, CHUNK], F32, "r0a")[:], placed([P, 1, CHUNK], F32, "r0b", 11264)[:]
         project(1, on_vector, r0[0], [(0, 0), (0, 1)])
         project(2, on_vector, r0[1], [(0, 2)])
         quantize_h(0, CHUNK, hs[:, :CHUNK], hb0[:])
-        hb1 = placed([P, PACK * CHUNK], BF16, "hb1", 6144)
-        gain_on_gpsimd(hb1[:, 320:], e1[:, 320:])
-        r_last = held([P, 7, CHUNK], F32, "r_last", "plane3")
-        r1 = placed([P, 2, CHUNK], F32, "r1a", 10240)[:], r_last[:, 6:]
-        project(3, on_vector, r1[0], [(256, 0), (256, 1)])
-        project(4, on_scalar, r1[1], [(256, 2)])
-        gain_on_vector(hb1[:, :320], e1[:, :320])
-        hb2 = placed([P, PACK * CHUNK], BF16, "hb2", 8192)
+        gather_words(896, held([P, SUB], U32, "vw896", "e0"))
+        hb1 = placed([P, PACK * CHUNK], BF16, "hb1", 13312)
+        gain_on_gpsimd(hb1[:, 256:], e1[:, 256:])
+        r1a = held([P, 2, CHUNK], F32, "r1a")
+        project(3, on_vector, r1a[:], [(256, 0), (256, 1)])
+        gain_on_vector(hb1[:, :256], e1[:, :256])
+        finish(0, 1, 2, r0[1], hs[:, :CHUNK], held([P, 1, CHUNK], F32, "ob0b")[:])
+        distance(896, 0, absd[3][:, halves[1]])
+        for half in halves:
+            decay(e3[:, half], absd[3][:, half])
+        hb2 = placed([P, PACK * CHUNK], BF16, "hb2", 11264)
         for half in halves:
             gain_on_vector(hb2[:, half], e2[:, half])
         hs1 = held([P, CHUNK], U8, "hs1", "e2")
         quantize_h(256, CHUNK, hs1[:], hb1[:])
         quantize_h(512, CHUNK, hs[:, 512:768], hb2[:])
-        hb3 = placed([P, PACK * SUB], BF16, "hb3", 7680)
-        gain_on_gpsimd(hb3[:], e3[:, : PACK * SUB])
-        finish(0, (1, 2), r0, hs[:, :CHUNK], placed([P, N_TILES, CHUNK], F32, "ob0", 3584))
-        finish(256, (5, 3), r1, hs1[:])
-        hb4 = placed([P, PACK * SUB], BF16, "hb4", 10240)
-        gain_on_vector(hb4[:], e3[:, PACK * SUB :])
-        quantize_h(768, SUB, hs[:, 768:896], hb3[:])
-        quantize_h(896, SUB, hs[:, 896:], hb4[:])
+        finish(0, 0, 1, r0[0], hs[:, :CHUNK], placed([P, 2, CHUNK], F32, "ob0a", 14336)[:])
+        r_last = held([P, 7, CHUNK], F32, "r_last", "plane3")
+        r1 = r1a[:], r_last[:, 6:]
+        project(3, on_scalar, r1[1], [(256, 2)])
+        hb3 = placed([P, PACK * CHUNK], BF16, "hb3", 12288)
+        gain_on_gpsimd(hb3[:, halves[0]], e3[:, halves[0]])
+        gain_on_vector(hb3[:, halves[1]], e3[:, halves[1]])
+        finish_both(256, (5, 2), r1, hs1[:])
+        quantize_h(768, CHUNK, hs[:, 768:], hb3[:])
         r2, r3 = (r_last[:, 0:2], r_last[:, 2:3]), (r_last[:, 4:6], r_last[:, 3:4])
-        project(6, on_scalar, r_last[:, 0:2], [(512, 0), (512, 1)])
         project(0, on_scalar, r_last[:, 2:4], [(512, 2), (768, 2)])
+        project(6, on_scalar, r_last[:, 0:2], [(512, 0), (512, 1)])
         project(1, on_scalar, r_last[:, 4:6], [(768, 0), (768, 1)])
-        finish(512, (4, 2), r2, hs[:, 512:768], placed([P, N_TILES, CHUNK], F32, "ob512", 7168))
-        finish(768, (5, 3), r3, hs[:, 768:])
+        finish_both(512, (4, 0), r2, hs[:, 512:768], "e3")
+        finish_both(768, (5, 6), r3, hs[:, 768:])

from contextlib import ExitStack

import concourse.mybir as mybir
from concourse.masks import make_identity

K, C, T, S, H, N = 1024, 512, 2048, 1024, 512, 384
FLOPS = 2 * S * (K * H + C * H + K * N + H * N)

F32 = mybir.dt.float32
BF16 = mybir.dt.bfloat16
I32 = mybir.dt.int32
U32 = mybir.dt.uint32
U16 = mybir.dt.uint16
U8 = mybir.dt.uint8
FP8X4 = mybir.dt.float8_e4m3fn_x4
FP4X4 = mybir.dt.float4_e2m1fn_x4
MULT = mybir.AluOpType.mult
ACT = mybir.ActivationFunctionType

P = 128
PACK = 4
HALF = S // 2
CHUNK = 256
SUB = 128
N_TILES = N // P


def tile_list_template_contact_gate_kernel(
    tc, xT, wgt, offs2, tab_words, tab_scales, offs, w1, w2_words, w2_scales, w3, w4_words, w4_scales, gain, out
):
    nc = tc.nc
    with ExitStack() as ctx:
        keep = ctx.enter_context(tc.tile_pool(name="keep", bufs=1))
        turns = ctx.enter_context(tc.tile_pool(name="turns", bufs=1))
        psum = ctx.enter_context(tc.psum_pool(name="psum", bufs=1))
        on_vector, on_scalar = nc.vector.tensor_copy, nc.scalar.copy

        def held(shape, dtype, name, tag=None):
            return keep.tile(shape, dtype, name=name, tag=tag or name, align_bytes=64)

        def placed(shape, dtype, name, offset):
            return turns.tile(shape, dtype, name=name, offset=offset, align_bytes=64)

        def load_words(tile, rows):
            nc.sync.dma_start(out=tile.bitcast(I32), in_=rows.bitcast(I32))

        def load_scale_rows(plane, rows, q):
            load_words(plane[32 * q : 32 * q + 4, :], rows[4 * q : 4 * q + 4, :])

        def quantize(codes, scales, values):
            nc.vector.quantize_mx(out=codes.bitcast(FP8X4), scales=scales, in_=values)

        def interleave(copy, dst, src):
            copy(
                out=dst.rearrange("p (c e i) -> p c i e", e=4, i=PACK),
                in_=src.rearrange("p i (c e) -> p c i e", e=4),
            )

        def interleave_dealt(copy, dst, src):
            copy(
                out=dst.rearrange("p (t m i) -> p m i t", t=PACK, i=PACK),
                in_=src.rearrange("p i (m t) -> p m i t", t=PACK),
            )

        def deal(dst, src):
            on_vector(out=dst.rearrange("p (t m) -> p t m", t=PACK), in_=src.rearrange("p (m t) -> p t m", t=PACK))

        def mm(acc, lhs, rhs, start, stop):
            nc.tensor.matmul_mx(out=acc, lhsT=lhs[0], lhsT_scale=lhs[1], rhs=rhs[0], rhs_scale=rhs[1], start=start, stop=stop)

        offs_sb = held([P, S // 16], U16, "offs_sb")
        offs2_sb = held([P, S // 16], U16, "offs2_sb")
        tabw = placed([P, T], U32, "tabw", 14336)
        tabs = held([P, T], U8, "tabs")
        wgt_rows = held([P, P], F32, "wgt_rows")
        wgt_sb = held([P, S], F32, "wgt_sb")
        planes = [held([P, T], F32, f"plane{u}") for u in range(8)]
        w1_raw = [placed([P, PACK, H], F32, "w1_raw0", 6144), held([P, PACK, H], F32, "w1_raw1")]
        w3_raw = held([P, 2, PACK, N], F32, "w3_raw")
        w2w_raw = held([P, 2 * H], U8, "w2w_raw")
        w2s_raw = held([P, H], U8, "w2s_raw")
        w2w = held([P, 2 * H], U8, "w2w")
        w4w = held([P, N], U32, "w4w")
        w4s = held([P, N], U8, "w4s")
        gain_row = held([P, PACK * CHUNK], F32, "gain_row")
        ident = held([P, P], F32, "ident")
        vs_rows = held([P, S], U8, "vs_rows")
        vs = held([P, S], U8, "vs")

        nc.gpsimd.memset(tabs[:].bitcast(I32), 0)
        make_identity(nc, ident[:])
        for plane in (w2s_raw, w4s, vs):
            nc.gpsimd.memset(plane[:].bitcast(I32), 0)

        x_rows = xT.rearrange("(a p i) t -> a i p t", a=2, i=PACK)
        w1_rows = w1.rearrange("(a p i) r -> a p i r", a=2, i=PACK)
        w3_rows = w3.rearrange("(a p i) n -> a p i n", a=2, i=PACK)

        def load_plane(u):
            nc.sync.dma_start(out=planes[u][:], in_=x_rows[u // PACK, u % PACK])

        nc.sync.dma_start(out=wgt_rows[:], in_=wgt.rearrange("(g r) (b j) -> g (r b) j", r=16, j=P)[:, :16, :])
        load_words(w2w_raw[:], w2_words[0])
        nc.sync.dma_start(offs_sb[:], offs)
        load_words(tabs[:16, :], tab_scales[0])
        load_plane(0)
        deal(w2w[:].bitcast(U16), w2w_raw[:].bitcast(U16))
        on_vector(vs_rows[:], tabs[:].indirect(offs_sb[:]))
        nc.sync.dma_start(offs2_sb[:], offs2)

        turned = psum.tile([P, P], F32, name="turned", tag="bank6")
        nc.tensor.transpose(turned[:], wgt_rows[:], ident[:])
        spreads = [held([P, 4, P], F32, f"spread{h}") for h in range(2)]
        for h, spread in enumerate(spreads):
            on_scalar(
                out=spread[:].rearrange("j b (q e) -> j b q e", e=8),
                in_=turned[:].rearrange("j (q b) -> j b q", b=8)[:, 4 * h : 4 * h + 4, :].unsqueeze(3).to_broadcast([P, 4, 16, 8]),
            )
            back = psum.tile([P, 4, P], F32, name="back", tag=f"bank{4 + h}")
            for b in range(4):
                nc.tensor.transpose(back[:, b, :], spread[:, b, :], ident[:])
            on_scalar(out=wgt_sb[:, HALF * h : HALF * (h + 1)], in_=back[:].rearrange("p b j -> p (b j)"))

        load_plane(1)
        gain_line = spreads[0][:].rearrange("j b p -> j (b p)")
        nc.sync.dma_start(out=gain_line[:1, :], in_=gain.unsqueeze(0))
        load_scale_rows(w2s_raw, w2_scales[0], 0)
        load_scale_rows(w2s_raw, w2_scales[0], 1)
        load_plane(2)
        load_scale_rows(w2s_raw, w2_scales[0], 2)
        load_scale_rows(w2s_raw, w2_scales[0], 3)
        load_plane(3)
        load_plane(4)
        nc.sync.dma_start(out=w1_raw[0][:], in_=w1_rows[0])
        load_plane(5)
        load_plane(6)
        nc.sync.dma_start(out=w1_raw[1][:], in_=w1_rows[1])
        load_plane(7)
        load_words(tabw[:], tab_words[0].rearrange("p t i -> p (t i)"))
        nc.sync.dma_start(out=w3_raw[:, 0], in_=w3_rows[0])
        load_scale_rows(vs, vs_rows, 0)
        load_scale_rows(vs, vs_rows, 1)
        load_scale_rows(vs, vs_rows, 2)
        load_scale_rows(vs, vs_rows, 3)
        nc.sync.dma_start(out=w3_raw[:, 1], in_=w3_rows[1])
        load_words(w4w[:], w4_words[0].rearrange("p n i -> p (n i)"))
        for q in range(4):
            load_scale_rows(w4s, w4_scales[0], q)

        gain_bank = psum.tile([P, P + PACK], F32, name="gain_bank")
        for t in range(PACK):
            nc.tensor.transpose(gain_bank[:, t : t + P], gain_line[:, t::PACK], ident[:])
        on_scalar(
            out=gain_row[:].rearrange("p (j t) -> p j t", t=PACK),
            in_=gain_bank[:, :PACK].unsqueeze(1).to_broadcast([P, CHUNK, PACK]),
        )

        picked = [held([P, PACK, S], F32, f"picked{a}") for a in range(2)]
        xq = [held([P, S], U32, f"xq{a}") for a in range(2)]
        w1q = [held([P, H], U32, f"w1q{a}") for a in range(2)]
        w1b = [held([P, PACK * H], BF16, f"w1b{a}") for a in range(2)]
        w3q = held([P, 2 * N], U32, "w3q")
        w3s = held([P, 2 * N], U8, "w3s")
        xs1 = held([P, 768], U8, "xs1")
        xs1_last = []
        hq = held([P, S], U32, "hq")
        vw = {}
        out_rows = out.rearrange("(m p) j -> p m j", p=P)

        def gather_x(u, j, width):
            lists = offs2_sb[:, j // 16 : (j + width) // 16]
            dst = picked[u // PACK][:, u % PACK, j : j + width]
            nc.vector.tensor_tensor(dst, planes[u][:].indirect(lists), wgt_sb[:, j : j + width], MULT)

        def gather_words(j, words):
            width = words.shape[1]
            on_vector(words[:], tabw[:].indirect(offs_sb[:, j // 16 : (j + width) // 16]))
            for s in range(0, width, SUB):
                vw[j + s] = words[:, s : s + SUB]

        def round_x(copy, a, j, width, tag=None):
            rounded = held([P, PACK * width], BF16, f"xb{a}_{j}", tag)
            interleave(copy, rounded[:], picked[a][:, :, j : j + width])
            return rounded

        def round_pair(copy, rounded, a, u, j, width):
            copy(
                out=rounded[:].rearrange("p (c i) -> p c i", i=PACK)[:, :, 2 * u : 2 * u + 2],
                in_=picked[a][:, 2 * u : 2 * u + 2, j : j + width].rearrange("p i c -> p c i"),
            )

        def x_scales(a, j, width):
            if a == 1:
                return xs1[:, j : j + width] if j < 768 else xs1_last[0][:, j - 768 : j - 768 + width]
            return xs0[j // HALF][:, j % HALF : j % HALF + width]

        def quantize_x(a, j, width, rounded):
            quantize(xq[a][:, j : j + width], x_scales(a, j, width), rounded[:])

        def round_w3_rest():
            on_vector(
                out=w3b_rest[:].rearrange("p (a c e i) -> p a c i e", a=2, e=4, i=PACK),
                in_=w3_raw[:, :, :, 256:].rearrange("p a i (c e) -> p a c i e", e=4),
            )

        def quantize_w3(j, width, rounded):
            quantize(w3q[:, j : j + width], w3s[:, j : j + width], rounded[:])

        def x_operand(a, cols):
            return xq[a][:, cols].bitcast(FP8X4), x_scales(a, cols.start, cols.stop - cols.start)

        def d_weights(k, t):
            if k == 2:
                return w2w[:, 2 * t * P : 2 * (t + 1) * P].bitcast(FP4X4), w2s[:, t * P : (t + 1) * P]
            return w1q[k][:, t * P : (t + 1) * P].bitcast(FP8X4), w1s[k][:, t * P : (t + 1) * P]

        def distance(j, bank, absd):
            cols = slice(j, j + SUB)
            d = psum.tile([P, PACK, SUB], F32, name="d", tag=f"bank{bank}")
            rhs = [x_operand(0, cols), x_operand(1, cols), (vw[j].bitcast(FP8X4), vs[:, cols])]
            order = (0, 1, 2) if j < CHUNK or j == S - SUB else (0, 2, 1)
            for n, k in enumerate(order):
                for t in range(PACK):
                    mm(d[:, t, :], d_weights(k, t), rhs[k], n == 0 and t == 0, n == 2 and t == PACK - 1)
            nc.scalar.activation(out=absd.rearrange("p (j t) -> p j t", t=PACK), in_=d[:].rearrange("p t j -> p j t"), func=ACT.Abs)

        def decay(e, absd):
            nc.scalar.activation(out=e, in_=absd, func=ACT.Exp, scale=-1.0)

        def gain_on_vector(dst, e):
            nc.vector.tensor_tensor(
                dst.rearrange("p (j t) -> p j t", t=PACK),
                e.rearrange("p (j t) -> p j t", t=PACK),
                gain_bank[:, :PACK].unsqueeze(1).to_broadcast([P, e.shape[1] // PACK, PACK]),
                MULT,
            )

        def gain_on_gpsimd(dst, e):
            nc.gpsimd.tensor_tensor(dst, e, gain_row[:, : e.shape[1]], MULT)

        def quantize_h(j, width, scales, rounded):
            quantize(hq[:, j : j + width], scales, rounded)

        parts = [range(0, 2), range(2, N_TILES)]

        def project(bank, copy, r_sb, pieces):
            r = psum.tile([P, len(pieces), CHUNK], F32, name="r", tag=f"bank{bank}")
            for n, (j0, m) in enumerate(pieces):
                for a in range(2):
                    first = 256 * a + P * m if m < 2 else 512 + P * a
                    w = slice(first, first + P)
                    mm(r[:, n, :], (w3q[:, w].bitcast(FP8X4), w3s[:, w]), x_operand(a, slice(j0, j0 + CHUNK)), a == 0, a == 1)
            copy(out=r_sb, in_=r[:])

        def finish(j0, part, bank, r_sb, scales, ob):
            cols, rows = slice(j0, j0 + CHUNK), parts[part]
            y = psum.tile([P, len(rows), CHUNK], F32, name="y", tag=f"bank{bank}")
            for m in rows:
                w = slice(m * P, (m + 1) * P)
                rhs = hq[:, cols].bitcast(FP8X4), scales
                mm(y[:, m - rows.start, :], (w4w[:, w].bitcast(FP8X4), w4s[:, w]), rhs, True, True)
            nc.vector.tensor_tensor(ob, y[:], r_sb, MULT)
            nc.sync.dma_start(out=out_rows[:, rows.start : rows.stop, cols], in_=ob)

        def finish_both(j0, banks, projected, scales, tag=None):
            staged = held([P, N_TILES, CHUNK], F32, f"ob{j0}", tag)
            for part, rows in enumerate(parts):
                finish(j0, part, banks[part], projected[part], scales, staged[:, rows.start : rows.stop])

        for h in range(2):
            gather_x(0, HALF * h, HALF)
        for u in range(1, PACK - 1):
            gather_x(u, 0, S)
        for h in range(2):
            gather_x(PACK - 1, HALF * h, HALF)
        w3b = placed([P, PACK * 512], BF16, "w3b", 0)
        w3b_rest = placed([P, PACK * 256], BF16, "w3b_rest", 4096)
        xb0 = [held([P, PACK * HALF], BF16, f"xb0_{h}", f"plane{h}") for h in range(2)]
        for u in range(2):
            for h in range(2):
                round_pair(on_scalar, xb0[h], 0, u, HALF * h, HALF)
        interleave_dealt(on_scalar, w1b[0][:], w1_raw[0][:])
        gather_x(4, 0, S)
        behind4 = held([P, H + HALF], U8, "behind4", "plane4")
        w2s = behind4[:, :H]
        deal(w2s, w2s_raw[:])
        xs0 = [behind4[:, H:]]
        quantize_x(0, 0, HALF, xb0[0])
        gather_x(5, HALF, HALF)
        gather_x(5, 0, HALF)
        xb1_paired = placed([P, PACK * (HALF + CHUNK)], BF16, "xb1_paired", 8192)
        xb1_last, xb1_first = xb1_paired[:, : PACK * HALF], xb1_paired[:, PACK * HALF :]
        round_pair(on_scalar, xb1_last, 1, 0, HALF, HALF)
        round_pair(on_scalar, xb1_first, 1, 0, 0, CHUNK)
        interleave_dealt(on_scalar, w1b[1][:], w1_raw[1][:])
        gather_x(6, 0, S)
        behind6 = held([P, H + HALF], U8, "behind6", "plane6")
        xs0.append(behind6[:, H:])
        w1s = [behind6[:, :H]]
        quantize_x(0, HALF, HALF, xb0[1])
        quantize(w1q[0][:], w1s[0][:], w1b[0][:])
        gather_x(7, 0, CHUNK)
        gather_x(7, CHUNK, CHUNK)
        gather_x(7, HALF, HALF)
        round_pair(on_scalar, xb1_first, 1, 1, 0, CHUNK)
        xb1 = [xb1_first, round_x(on_scalar, 1, CHUNK, CHUNK)]
        round_pair(on_scalar, xb1_last, 1, 1, HALF, HALF)
        w1s.append(held([P, H], U8, "w1s1", "plane7"))
        quantize(w1q[1][:], w1s[1][:], w1b[1][:])
        quantize_x(1, 0, CHUNK, xb1[0])
        gather_words(0, held([P, CHUNK], U32, "vw0"))
        quantize_x(1, CHUNK, CHUNK, xb1[1])
        gather_words(CHUNK, held([P, CHUNK], U32, "vw256", "w1b1"))
        gather_words(HALF, held([P, CHUNK], U32, "vw512", "xb1_256"))
        quantize_x(1, HALF, CHUNK, xb1_last[:, : PACK * CHUNK])
        for a, copy in enumerate((on_scalar, on_vector)):
            interleave(copy, w3b[:, PACK * 256 * a : PACK * 256 * (a + 1)], w3_raw[:, a, :, :256])
        round_w3_rest()
        quantize_w3(0, 512, w3b)
        quantize_w3(512, 256, w3b_rest)
        gather_words(768, placed([P, SUB], U32, "vw768", 256))
        xs1_last.append(placed([P, CHUNK], U8, "xs1_last", 0))
        quantize_x(1, 768, CHUNK, xb1_last[:, PACK * CHUNK :])
        absd = [held([P, CHUNK * PACK], F32, f"absd{c}", f"plane{c}") for c in range(4)]
        e0, e1, e2, e3 = decayed = [held([P, CHUNK * PACK], F32, f"e{c}") for c in range(4)]
        halves = [slice(0, PACK * SUB), slice(PACK * SUB, PACK * CHUNK)]
        for c in range(3):
            for s in range(2):
                distance(CHUNK * c + SUB * s, 2 * c + s, absd[c][:, halves[s]])
            for half in halves:
                decay(decayed[c][:, half], absd[c][:, half])
        distance(768, 6, absd[3][:, halves[0]])
        hs = held([P, S], U8, "hs")
        hb0 = placed([P, PACK * CHUNK], BF16, "hb0", 12288)
        gain_on_vector(hb0[:, :512], e0[:, :512])
        gain_on_gpsimd(hb0[:, 512:], e0[:, 512:])
        r0 = held([P, 2, CHUNK], F32, "r0a")[:], placed([P, 1, CHUNK], F32, "r0b", 11264)[:]
        project(1, on_vector, r0[0], [(0, 0), (0, 1)])
        project(2, on_vector, r0[1], [(0, 2)])
        quantize_h(0, CHUNK, hs[:, :CHUNK], hb0[:])
        gather_words(896, held([P, SUB], U32, "vw896", "e0"))
        hb1 = placed([P, PACK * CHUNK], BF16, "hb1", 13312)
        gain_on_gpsimd(hb1[:, 256:], e1[:, 256:])
        r1a = held([P, 2, CHUNK], F32, "r1a")
        project(3, on_vector, r1a[:], [(256, 0), (256, 1)])
        gain_on_vector(hb1[:, :256], e1[:, :256])
        finish(0, 1, 2, r0[1], hs[:, :CHUNK], held([P, 1, CHUNK], F32, "ob0b")[:])
        distance(896, 0, absd[3][:, halves[1]])
        for half in halves:
            decay(e3[:, half], absd[3][:, half])
        hb2 = placed([P, PACK * CHUNK], BF16, "hb2", 11264)
        for half in halves:
            gain_on_vector(hb2[:, half], e2[:, half])
        hs1 = held([P, CHUNK], U8, "hs1", "e2")
        quantize_h(256, CHUNK, hs1[:], hb1[:])
        quantize_h(512, CHUNK, hs[:, 512:768], hb2[:])
        finish(0, 0, 1, r0[0], hs[:, :CHUNK], placed([P, 2, CHUNK], F32, "ob0a", 14336)[:])
        r_last = held([P, 7, CHUNK], F32, "r_last", "plane3")
        r1 = r1a[:], r_last[:, 6:]
        project(3, on_scalar, r1[1], [(256, 2)])
        hb3 = placed([P, PACK * CHUNK], BF16, "hb3", 12288)
        gain_on_gpsimd(hb3[:, halves[0]], e3[:, halves[0]])
        gain_on_vector(hb3[:, halves[1]], e3[:, halves[1]])
        finish_both(256, (5, 2), r1, hs1[:])
        quantize_h(768, CHUNK, hs[:, 768:], hb3[:])
        r2, r3 = (r_last[:, 0:2], r_last[:, 2:3]), (r_last[:, 4:6], r_last[:, 3:4])
        project(0, on_scalar, r_last[:, 2:4], [(512, 2), (768, 2)])
        project(6, on_scalar, r_last[:, 0:2], [(512, 0), (512, 1)])
        project(1, on_scalar, r_last[:, 4:6], [(768, 0), (768, 1)])
        finish_both(512, (4, 0), r2, hs[:, 512:768], "e3")
        finish_both(768, (5, 6), r3, hs[:, 768:])
